import numpy as np
import ml_dtypes


def mxq(x, axis, fmt="e4m3"):
    dtype, down = {"e4m3": (ml_dtypes.float8_e4m3fn, 7), "e5m2": (ml_dtypes.float8_e5m2, 14)}[fmt]
    v = np.moveaxis(np.asarray(x, np.float32).astype(ml_dtypes.bfloat16).astype(np.float64), axis, -1)
    blocks = v.reshape(v.shape[:-1] + (-1, 32))
    amax = np.abs(blocks).max(-1, keepdims=True)
    byte = np.maximum(np.where(amax > 0, np.frexp(amax)[1] - 1 + 127, 0) - down, 1)
    scale = np.exp2(byte - 127.0)
    codes = (blocks / scale).astype(np.float32).astype(dtype).astype(np.float64)
    return np.moveaxis((codes * scale).reshape(v.shape), -1, axis)


WIDE = False


def mx_kscale(k):
    if not WIDE:
        return np.ones(k)
    levels = np.array([10, -10, 5, -5, 0])
    if k % 512:
        return np.exp2(np.random.permutation(np.resize(levels, k // 32))).repeat(32)
    a = np.empty((k // 512, 16))
    for p in range(k // 512):
        a[p, :8] = np.random.permutation(np.resize(levels, 8))
        for g in range(8):
            far = levels[np.abs(levels - a[p, g]) >= 10]
            a[p, g + 8] = far[np.random.randint(len(far))]
    return np.exp2(a.ravel()).repeat(32)


def f64(x):
    return np.asarray(x).astype(np.float64)


def planes(y):
    n, m = y.shape
    v = y.astype(np.float32).astype(ml_dtypes.bfloat16).astype(np.float64).reshape(n // 32, 32, m)
    top = np.abs(v).max(1)
    byte = np.clip(np.where(top > 0, np.frexp(top)[1] - 1 + 127 - 7, 1), 1, 254)
    codes = (v * np.exp2(127.0 - byte)[:, None, :]).reshape(n, m).astype(np.float32).astype(ml_dtypes.float8_e4m3fn).view(np.uint8)
    words = codes.reshape(n // 512, 128, 4, m).transpose(0, 1, 3, 2)
    return np.ascontiguousarray(words), np.ascontiguousarray(byte.astype(np.uint8).reshape(n // 512, 16, m))


def split(x):
    m, e = np.frexp(f64(x))
    hi = np.ldexp(np.trunc(16.0 * m) / 16.0, e)
    return hi, f64(x) - hi


K, M, T = 1024, 1536, 512


def setup_inputs():
    n = np.random.standard_normal
    s = mx_kscale(K)[:, None]
    return {
        "w": (n((K, M)) / np.sqrt(K) / s).astype(np.float32),
        "x": (n((K, T)) * s).astype(np.float32),
        "b": (0.3 * n(1536)).astype(np.float32),
    }


def reference(w, x, b):
    w_hi, w_lo = split(w)
    w_hi_, w_lo_ = mxq(w_hi, 0, "e4m3"), mxq(w_lo, 0, "e4m3")
    x_ = mxq(f64(x), 0, "e4m3")
    y = x_.T @ w_hi_ + x_.T @ w_lo_
    out_0 = y + f64(b)[None, :]
    return (out_0,) + planes(out_0)

@@ -1,0 +1,267 @@
+from contextlib import ExitStack
+
+import concourse.mybir as mybir
+from concourse.masks import make_identity
+
+K, M, T = 1024, 1536, 512
+FLOPS = 2 * 2 * K * M * T
+
+F32 = mybir.dt.float32
+BF16 = mybir.dt.bfloat16
+I32 = mybir.dt.int32
+U32 = mybir.dt.uint32
+U8 = mybir.dt.uint8
+FP8X4 = mybir.dt.float8_e4m3fn_x4
+ALU = mybir.AluOpType
+
+P = 128
+PACK = 4
+K_PASS = P * PACK
+PASSES = K // K_PASS
+CHUNK = 256
+HI_MASK_PAIR = 0xFFF0FFF0 - (1 << 32)
+B_COLS = M // P
+
+W_LOADS = [(0, 0, 128), (0, 128, 128), (1, 0, 256), (0, 256, 256), (1, 256, 256),
+           (0, 512, 512), (1, 512, 512), (0, 1024, 512), (1, 1024, 512)]
+PIECES = [(0, 0, 128), (0, 128, 128), (1, 0, 256), (0, 256, 256), (1, 256, 256),
+          (0, 512, 256), (0, 768, 256), (1, 512, 256), (1, 768, 256),
+          (0, 1024, 256), (1, 1024, 256), (0, 1280, 256), (1, 1280, 128), (1, 1408, 128)]
+CHUNKS = [(0, 256), (256, 256), (512, 256), (768, 256), (1024, 256), (1280, 128), (1408, 128)]
+
+
+def tile_mix_hilo_tm_pl_bias_kernel(tc, w, x, b, out_0, out_1, out_2):
+    nc = tc.nc
+    out_rows = out_0.rearrange("(p r) n -> p r n", r=PACK)
+    out_words = out_1.rearrange("a p n i -> (a p) (n i)").bitcast(I32)
+    out_scales = out_2.rearrange("a q n -> (a q) n").bitcast(I32)
+
+    with ExitStack() as ctx:
+        keep = ctx.enter_context(tc.tile_pool(name="keep", bufs=1))
+        psum = ctx.enter_context(tc.psum_pool(name="psum", bufs=1))
+        ctx.enter_context(tc.manual_schedule())
+
+        ident = keep.tile([P, P], F32, name="ident")
+        b_col = keep.tile([P, B_COLS], F32, name="b_col")
+        bias = keep.tile([P, M], F32, name="bias")
+        w_raw = [keep.tile([P, PACK, wd], F32, name="w_raw%d" % i) for i, (g, c0, wd) in enumerate(W_LOADS)]
+        x_raw = [keep.tile([P, PACK, T], F32, name="x_raw%d" % g) for g in range(PASSES)]
+        x_bf = [keep.tile([P, PACK * T], BF16, name="x_bf%d" % g, align_bytes=64) for g in range(PASSES)]
+        x_codes = [keep.tile([P, T], U32, name="x_codes%d" % g, align_bytes=64) for g in range(PASSES)]
+        x_scales = [keep.tile([P, T], U8, name="x_scales%d" % g, align_bytes=64) for g in range(PASSES)]
+        hi_bf = [keep.tile([P, PACK * wd], BF16, name="hi_bf%d" % i, align_bytes=64) for i, (g, c0, wd) in enumerate(PIECES)]
+        lo_bf = [keep.tile([P, PACK * wd], BF16, name="lo_bf%d" % i, align_bytes=64) for i, (g, c0, wd) in enumerate(PIECES)]
+        w_codes = [[keep.tile([P, M], U32, name="w_codes%d_%d" % (g, h), align_bytes=64) for h in range(2)] for g in range(PASSES)]
+        w_scales = [[keep.tile([P, M], U8, name="w_scales%d_%d" % (g, h), align_bytes=64) for h in range(2)] for g in range(PASSES)]
+        y32 = [keep.tile([P, PACK, wd], F32, name="y32_%d" % i) for i, (c0, wd) in enumerate(CHUNKS)]
+        y_bf = [keep.tile([P, PACK * wd], BF16, name="y_bf%d" % i, align_bytes=64) for i, (c0, wd) in enumerate(CHUNKS)]
+        y_codes = [keep.tile([P, wd], U32, name="y_codes%d" % i, align_bytes=64) for i, (c0, wd) in enumerate(CHUNKS)]
+        y_scales = keep.tile([P, M], U8, name="y_scales", align_bytes=64)
+        acc = {}
+
+        def load_w(i):
+            g, c0, wd = W_LOADS[i]
+            rows = w[g * K_PASS:(g + 1) * K_PASS, c0:c0 + wd]
+            nc.sync.dma_start(out=w_raw[i][:], in_=rows.rearrange("(p j) n -> p j n", j=PACK))
+
+        def load_x(g):
+            rows = x[g * K_PASS:(g + 1) * K_PASS, :]
+            nc.sync.dma_start(out=x_raw[g][:], in_=rows.rearrange("(p j) t -> p j t", j=PACK))
+
+        def raw_of(i):
+            g, c0, wd = PIECES[i]
+            for k, (lg, l0, lw) in enumerate(W_LOADS):
+                if lg == g and l0 <= c0 and c0 + wd <= l0 + lw:
+                    return w_raw[k], c0 - l0, wd
+            raise ValueError("no load")
+
+        def paired(tile_bf):
+            return tile_bf[:].rearrange("p (c i j) -> p c j i", i=2, j=PACK)
+
+        def upper(i):
+            raw, o, wd = raw_of(i)
+            halves = raw[:].bitcast(BF16)[:, :, 2 * o:2 * (o + wd)].rearrange("p j (c i h) -> p c j i h", i=2, h=2)
+            nc.scalar.copy(out=paired(hi_bf[i]), in_=halves[:, :, :, :, 1])
+
+        def mask(i):
+            words = hi_bf[i][:].bitcast(I32)
+            nc.vector.tensor_scalar(out=words, in0=words, scalar1=HI_MASK_PAIR, scalar2=None, op0=ALU.bitwise_and)
+
+        def lower(i):
+            raw, o, wd = raw_of(i)
+            src = raw[:, :, o:o + wd].rearrange("p j (c i) -> p c j i", i=2)
+            nc.vector.tensor_tensor(out=paired(lo_bf[i]), in0=src, in1=paired(hi_bf[i]), op=ALU.subtract)
+
+        def quant_w(i, h):
+            g, c0, wd = PIECES[i]
+            src = (hi_bf, lo_bf)[h][i]
+            nc.vector.quantize_mx(out=w_codes[g][h][:, c0:c0 + wd].bitcast(FP8X4),
+                                  scales=w_scales[g][h][:, c0:c0 + wd], in_=src[:])
+
+        def cast_x(g, half):
+            dst = x_bf[g][:].rearrange("p (u v m j) -> p u m j v", u=2, v=2, j=PACK)
+            src = x_raw[g][:].rearrange("p j (m u v) -> p u m j v", u=2, v=2)
+            nc.scalar.copy(out=dst[:, half], in_=src[:, half])
+
+        def quant_x(g):
+            nc.vector.quantize_mx(out=x_codes[g][:].bitcast(FP8X4), scales=x_scales[g][:], in_=x_bf[g][:])
+
+        def banks_of(c):
+            c0, wd = CHUNKS[c]
+            return PACK * wd // 512
+
+        def bank_name(c, u):
+            first = sum(banks_of(k) for k in range(c))
+            return "bank%d" % ((first + u) % 8)
+
+        def matmuls(c):
+            c0, wd = CHUNKS[c]
+            per_bank = 512 // wd
+            for u in range(banks_of(c)):
+                tile_acc = psum.tile([P, per_bank, wd], F32, name="acc%d_%d" % (c, u), tag=bank_name(c, u))
+                acc[(c, u)] = tile_acc
+                for v in range(per_bank):
+                    r = u * per_bank + v
+                    steps = [(g, h) for g in range(PASSES) for h in range(2)]
+                    for s, (g, h) in enumerate(steps):
+                        nc.tensor.matmul_mx(
+                            out=tile_acc[:, v, :],
+                            lhsT=x_codes[g][:, r * P:(r + 1) * P].bitcast(FP8X4),
+                            lhsT_scale=x_scales[g][:, r * P:(r + 1) * P],
+                            rhs=w_codes[g][h][:, c0:c0 + wd].bitcast(FP8X4),
+                            rhs_scale=w_scales[g][h][:, c0:c0 + wd],
+                            start=(s == 0), stop=(s == len(steps) - 1))
+
+        def drain(c, u):
+            c0, wd = CHUNKS[c]
+            per_bank = 512 // wd
+            nc.vector.tensor_tensor(
+                out=y32[c][:, u * per_bank:(u + 1) * per_bank, :], in0=acc[(c, u)][:],
+                in1=bias[:, c0:c0 + wd].unsqueeze(1).to_broadcast([P, per_bank, wd]), op=ALU.add)
+
+        def store_y(c):
+            c0, wd = CHUNKS[c]
+            nc.sync.dma_start(out=out_rows[:, :, c0:c0 + wd], in_=y32[c][:])
+
+        def cast_y(c):
+            src = y32[c][:].rearrange("p r (c i) -> p c r i", i=2)
+            nc.scalar.copy(out=paired(y_bf[c]), in_=src)
+
+        def quant_y(c):
+            c0, wd = CHUNKS[c]
+            nc.vector.quantize_mx(out=y_codes[c][:].bitcast(FP8X4), scales=y_scales[:, c0:c0 + wd], in_=y_bf[c][:])
+
+        def store_words(c, eng):
+            c0, wd = CHUNKS[c]
+            eng.dma_start(out=out_words[:, c0:c0 + wd], in_=y_codes[c][:].bitcast(I32))
+
+        def store_scales(c0, c1, engs):
+            for q in range(4):
+                engs[q % len(engs)].dma_start(
+                    out=out_scales[4 * q:4 * q + 4, c0 // 4:c1 // 4],
+                    in_=y_scales[32 * q:32 * q + 4, c0:c1].bitcast(I32))
+
+        def spread_bias(u):
+            spread = psum.tile([P, 4, P], F32, name="spread%d" % u, tag="bank%d" % (5 + u))
+            for v in range(4):
+                col = 4 * u + v
+                nc.tensor.transpose(spread[:, v, :], b_col[:, col:col + 1].to_broadcast([P, P]), ident[:])
+            acc[("b", u)] = spread
+
+        def copy_bias(u):
+            dst = bias[:].rearrange("q (p c) -> q p c", c=B_COLS)[:, :, 4 * u:4 * u + 4]
+            nc.scalar.copy(out=dst, in_=acc[("b", u)][:].rearrange("q v p -> q p v"))
+
+        load_w(0)
+        load_w(1)
+        nc.sync.dma_start(out=b_col[:], in_=b.rearrange("(p c) -> p c", c=B_COLS))
+        for i in (2, 3, 4):
+            load_w(i)
+        load_x(0)
+        load_w(5)
+        load_x(1)
+        for i in (6, 7, 8):
+            load_w(i)
+        make_identity(nc, ident[:])
+        for u in range(3):
+            spread_bias(u)
+
+        def extras_s(i):
+            if i == 2:
+                copy_bias(0)
+            if i == 3:
+                copy_bias(1)
+                copy_bias(2)
+            if i == 4:
+                cast_x(0, 0)
+                cast_x(0, 1)
+            if i == 6:
+                cast_x(1, 0)
+                cast_x(1, 1)
+
+        def finish(c):
+            for u in range(banks_of(c)):
+                drain(c, u)
+            store_y(c)
+
+        def planes(c):
+            quant_y(c)
+            store_words(c, nc.sync)
+
+        n = len(PIECES)
+        upper(0)
+        upper(1)
+        mask(0)
+        quant_w(0, 0)
+        for i in range(n):
+            if i + 2 < n:
+                upper(i + 2)
+                extras_s(i + 2)
+            lower(i)
+            if i == 4:
+                quant_x(0)
+            if i == 6:
+                quant_x(1)
+                matmuls(0)
+                matmuls(1)
+            if i + 1 < n:
+                mask(i + 1)
+            else:
+                planes(4)
+            quant_w(i, 1)
+            if i + 1 < n:
+                quant_w(i + 1, 0)
+            if i == 7:
+                matmuls(2)
+                finish(0)
+                cast_y(0)
+            if i == 8:
+                matmuls(3)
+                finish(1)
+                cast_y(1)
+                planes(0)
+            if i == 9:
+                finish(2)
+                cast_y(2)
+                planes(1)
+            if i == 10:
+                matmuls(4)
+                finish(3)
+                cast_y(3)
+                planes(2)
+            if i == 11:
+                planes(3)
+                store_scales(0, 1024, [nc.sync])
+                finish(4)
+                cast_y(4)
+            if i == 12:
+                matmuls(5)
+        matmuls(6)
+        finish(5)
+        cast_y(5)
+        finish(6)
+        cast_y(6)
+        planes(5)
+        quant_y(6)
+        store_words(6, nc.scalar)
+        store_scales(1024, M, [nc.sync, nc.scalar])

@@ -13,21 +13,20 @@ U32 = mybir.dt.uint32
 U8 = mybir.dt.uint8
 FP8X4 = mybir.dt.float8_e4m3fn_x4
 ALU = mybir.AluOpType
+ACT = mybir.ActivationFunctionType
 
 P = 128
 PACK = 4
 K_PASS = P * PACK
 PASSES = K // K_PASS
-CHUNK = 256
 HI_MASK_PAIR = 0xFFF0FFF0 - (1 << 32)
 B_COLS = M // P
+BIAS0 = 512
 
-W_LOADS = [(0, 0, 128), (0, 128, 128), (1, 0, 256), (0, 256, 256), (1, 256, 256),
-           (0, 512, 512), (1, 512, 512), (0, 1024, 512), (1, 1024, 512)]
-PIECES = [(0, 0, 128), (0, 128, 128), (1, 0, 256), (0, 256, 256), (1, 256, 256),
-          (0, 512, 256), (0, 768, 256), (1, 512, 256), (1, 768, 256),
-          (0, 1024, 256), (1, 1024, 256), (0, 1280, 256), (1, 1280, 128), (1, 1408, 128)]
-CHUNKS = [(0, 256), (256, 256), (512, 256), (768, 256), (1024, 256), (1280, 128), (1408, 128)]
+W_LOADS = [(0, 0, 128), (0, 128, 128), (0, 256, 128), (0, 384, 128), (1, 0, 256), (1, 256, 256), (0, 512, 256), (1, 512, 256), (0, 768, 256), (1, 768, 256), (0, 1024, 256), (1, 1024, 256), (0, 1280, 256), (1, 1280, 256)]
+PIECES = [(0, 0, 128), (0, 128, 128), (0, 256, 128), (0, 384, 128), (1, 0, 256), (1, 256, 256), (0, 512, 256), (1, 512, 256), (0, 768, 256), (1, 768, 256), (0, 1024, 256), (1, 1024, 256), (0, 1280, 256), (1, 1280, 128), (1, 1408, 128)]
+Y_TILES = [(0, 256), (256, 256), (512, 256), (768, 256), (1024, 256), (1280, 128), (1408, 128)]
+PLANES = [(0, 512), (512, 512), (1024, 256), (1280, 128), (1408, 128)]
 
 
 def tile_mix_hilo_tm_pl_bias_kernel(tc, w, x, b, out_0, out_1, out_2):
@@ -42,22 +41,28 @@ def tile_mix_hilo_tm_pl_bias_kernel(tc, w, x, b, out_0, out_1, out_2):
         ctx.enter_context(tc.manual_schedule())
 
         ident = keep.tile([P, P], F32, name="ident")
+        b_rows = keep.tile([P, P], F32, name="b_rows")
         b_col = keep.tile([P, B_COLS], F32, name="b_col")
-        bias = keep.tile([P, M], F32, name="bias")
+        bias = keep.tile([P, M - BIAS0], F32, name="bias")
         w_raw = [keep.tile([P, PACK, wd], F32, name="w_raw%d" % i) for i, (g, c0, wd) in enumerate(W_LOADS)]
         x_raw = [keep.tile([P, PACK, T], F32, name="x_raw%d" % g) for g in range(PASSES)]
         x_bf = [keep.tile([P, PACK * T], BF16, name="x_bf%d" % g, align_bytes=64) for g in range(PASSES)]
         x_codes = [keep.tile([P, T], U32, name="x_codes%d" % g, align_bytes=64) for g in range(PASSES)]
         x_scales = [keep.tile([P, T], U8, name="x_scales%d" % g, align_bytes=64) for g in range(PASSES)]
-        hi_bf = [keep.tile([P, PACK * wd], BF16, name="hi_bf%d" % i, align_bytes=64) for i, (g, c0, wd) in enumerate(PIECES)]
-        lo_bf = [keep.tile([P, PACK * wd], BF16, name="lo_bf%d" % i, align_bytes=64) for i, (g, c0, wd) in enumerate(PIECES)]
-        w_codes = [[keep.tile([P, M], U32, name="w_codes%d_%d" % (g, h), align_bytes=64) for h in range(2)] for g in range(PASSES)]
-        w_scales = [[keep.tile([P, M], U8, name="w_scales%d_%d" % (g, h), align_bytes=64) for h in range(2)] for g in range(PASSES)]
-        y32 = [keep.tile([P, PACK, wd], F32, name="y32_%d" % i) for i, (c0, wd) in enumerate(CHUNKS)]
-        y_bf = [keep.tile([P, PACK * wd], BF16, name="y_bf%d" % i, align_bytes=64) for i, (c0, wd) in enumerate(CHUNKS)]
-        y_codes = [keep.tile([P, wd], U32, name="y_codes%d" % i, align_bytes=64) for i, (c0, wd) in enumerate(CHUNKS)]
+        w_bf = [keep.tile([P, 2, PACK * wd], BF16, name="w_bf%d" % i, align_bytes=64) for i, (g, c0, wd) in enumerate(PIECES)]
+        w_codes = [keep.tile([P, 2, wd], U32, name="w_codes%d" % i, align_bytes=64) for i, (g, c0, wd) in enumerate(PIECES)]
+        w_scales = [keep.tile([P, 2, wd], U8, name="w_scales%d" % i, align_bytes=64) for i, (g, c0, wd) in enumerate(PIECES)]
+        y32 = [keep.tile([P, PACK, wd], F32, name="y32_%d" % i) for i, (c0, wd) in enumerate(Y_TILES)]
+        y_bf = [keep.tile([P, PACK * wd], BF16, name="y_bf%d" % i, align_bytes=64) for i, (c0, wd) in enumerate(PLANES)]
+        y_codes = [keep.tile([P, wd], U32, name="y_codes%d" % i, align_bytes=64) for i, (c0, wd) in enumerate(PLANES)]
         y_scales = keep.tile([P, M], U8, name="y_scales", align_bytes=64)
-        acc = {}
+        held = {}
+
+        def holder(spans, g, c0, wd):
+            return [(k, c0 - s0) for k, (sg, s0, sw) in enumerate(spans) if sg == g and s0 <= c0 and c0 + wd <= s0 + sw][0]
+
+        def span(spans, c0, wd):
+            return [(k, c0 - s0) for k, (s0, sw) in enumerate(spans) if s0 <= c0 and c0 + wd <= s0 + sw][0]
 
         def load_w(i):
             g, c0, wd = W_LOADS[i]
@@ -68,35 +73,35 @@ def tile_mix_hilo_tm_pl_bias_kernel(tc, w, x, b, out_0, out_1, out_2):
             rows = x[g * K_PASS:(g + 1) * K_PASS, :]
             nc.sync.dma_start(out=x_raw[g][:], in_=rows.rearrange("(p j) t -> p j t", j=PACK))
 
-        def raw_of(i):
-            g, c0, wd = PIECES[i]
-            for k, (lg, l0, lw) in enumerate(W_LOADS):
-                if lg == g and l0 <= c0 and c0 + wd <= l0 + lw:
-                    return w_raw[k], c0 - l0, wd
-            raise ValueError("no load")
+        def load_b():
+            nc.sync.dma_start(out=b_rows[0:B_COLS, :], in_=b.rearrange("(c p) -> c p", p=P))
 
-        def paired(tile_bf):
-            return tile_bf[:].rearrange("p (c i j) -> p c j i", i=2, j=PACK)
+        def paired(ap):
+            return ap.rearrange("p (c i j) -> p c j i", i=2, j=PACK)
 
         def upper(i):
-            raw, o, wd = raw_of(i)
-            halves = raw[:].bitcast(BF16)[:, :, 2 * o:2 * (o + wd)].rearrange("p j (c i h) -> p c j i h", i=2, h=2)
-            nc.scalar.copy(out=paired(hi_bf[i]), in_=halves[:, :, :, :, 1])
+            g, c0, wd = PIECES[i]
+            k, o = holder(W_LOADS, g, c0, wd)
+            halves = w_raw[k][:].bitcast(BF16)[:, :, 2 * o:2 * (o + wd)].rearrange("p j (c i h) -> p c j i h", i=2, h=2)
+            nc.scalar.copy(out=paired(w_bf[i][:, 0, :]), in_=halves[:, :, :, :, 1])
 
         def mask(i):
-            words = hi_bf[i][:].bitcast(I32)
+            words = w_bf[i][:, 0, :].bitcast(I32)
             nc.vector.tensor_scalar(out=words, in0=words, scalar1=HI_MASK_PAIR, scalar2=None, op0=ALU.bitwise_and)
 
         def lower(i):
-            raw, o, wd = raw_of(i)
-            src = raw[:, :, o:o + wd].rearrange("p j (c i) -> p c j i", i=2)
-            nc.vector.tensor_tensor(out=paired(lo_bf[i]), in0=src, in1=paired(hi_bf[i]), op=ALU.subtract)
-
-        def quant_w(i, h):
             g, c0, wd = PIECES[i]
-            src = (hi_bf, lo_bf)[h][i]
-            nc.vector.quantize_mx(out=w_codes[g][h][:, c0:c0 + wd].bitcast(FP8X4),
-                                  scales=w_scales[g][h][:, c0:c0 + wd], in_=src[:])
+            k, o = holder(W_LOADS, g, c0, wd)
+            src = w_raw[k][:, :, o:o + wd].rearrange("p j (c i) -> p c j i", i=2)
+            nc.vector.tensor_tensor(out=paired(w_bf[i][:, 1, :]), in0=src, in1=paired(w_bf[i][:, 0, :]), op=ALU.subtract)
+
+        def quant_part(i, h):
+            nc.vector.quantize_mx(out=w_codes[i][:, h, :].bitcast(FP8X4), scales=w_scales[i][:, h, :], in_=w_bf[i][:, h, :])
+
+        def quant_both(i):
+            nc.vector.quantize_mx(out=w_codes[i][:].rearrange("p h n -> p (h n)").bitcast(FP8X4),
+                                  scales=w_scales[i][:].rearrange("p h n -> p (h n)"),
+                                  in_=w_bf[i][:].rearrange("p h n -> p (h n)"))
 
         def cast_x(g, half):
             dst = x_bf[g][:].rearrange("p (u v m j) -> p u m j v", u=2, v=2, j=PACK)
@@ -106,162 +111,262 @@ def tile_mix_hilo_tm_pl_bias_kernel(tc, w, x, b, out_0, out_1, out_2):
         def quant_x(g):
             nc.vector.quantize_mx(out=x_codes[g][:].bitcast(FP8X4), scales=x_scales[g][:], in_=x_bf[g][:])
 
-        def banks_of(c):
-            c0, wd = CHUNKS[c]
-            return PACK * wd // 512
+        def product(out, r, g, h, c0, wd):
+            k, o = holder(PIECES, g, c0, wd)
+            nc.tensor.matmul_mx(
+                out=out,
+                lhsT=x_codes[g][:, r * P:(r + 1) * P].bitcast(FP8X4),
+                lhsT_scale=x_scales[g][:, r * P:(r + 1) * P],
+                rhs=w_codes[k][:, h, o:o + wd].bitcast(FP8X4),
+                rhs_scale=w_scales[k][:, h, o:o + wd],
+                start=(g == 0 and h == 0), stop=(g == PASSES - 1 and h == 1))
 
-        def bank_name(c, u):
-            first = sum(banks_of(k) for k in range(c))
-            return "bank%d" % ((first + u) % 8)
+        def mm_turned(c0, g, bank):
+            k, o = holder(PIECES, g, c0, P)
+            if g == 0:
+                held[bank] = psum.tile([P, T], F32, name="sum_t%d" % c0, tag="bank%d" % bank)
+            for h in range(2):
+                nc.tensor.matmul_mx(
+                    out=held[bank][:],
+                    lhsT=w_codes[k][:, h, o:o + P].bitcast(FP8X4),
+                    lhsT_scale=w_scales[k][:, h, o:o + P],
+                    rhs=x_codes[g][:].bitcast(FP8X4),
+                    rhs_scale=x_scales[g][:],
+                    start=(g == 0 and h == 0), stop=(g == PASSES - 1 and h == 1))
 
-        def matmuls(c):
-            c0, wd = CHUNKS[c]
+        def drain_turned(c0, bank):
+            y_t = keep.tile([P, T], F32, name="y_t%d" % c0)
+            held[("y_t", c0)] = y_t
+            nc.scalar.activation(out=y_t[:], in_=held[bank][:], func=ACT.Identity,
+                                 bias=b_col[:, c0 // P:c0 // P + 1], scale=1.0)
+
+        def turn(c0, bank):
+            held[bank] = psum.tile([P, PACK, P], F32, name="turned%d" % c0, tag="bank%d" % bank)
+            for r in range(PACK):
+                nc.tensor.transpose(held[bank][:, r, :], held[("y_t", c0)][:, r * P:(r + 1) * P], ident[:])
+
+        def copy_turned(c0, bank):
+            k, o = span(Y_TILES, c0, P)
+            nc.scalar.copy(out=y32[k][:, :, o:o + P], in_=held[bank][:])
+
+        def mm_bank(c0, wd, bank, u):
             per_bank = 512 // wd
-            for u in range(banks_of(c)):
-                tile_acc = psum.tile([P, per_bank, wd], F32, name="acc%d_%d" % (c, u), tag=bank_name(c, u))
-                acc[(c, u)] = tile_acc
-                for v in range(per_bank):
-                    r = u * per_bank + v
-                    steps = [(g, h) for g in range(PASSES) for h in range(2)]
-                    for s, (g, h) in enumerate(steps):
-                        nc.tensor.matmul_mx(
-                            out=tile_acc[:, v, :],
-                            lhsT=x_codes[g][:, r * P:(r + 1) * P].bitcast(FP8X4),
-                            lhsT_scale=x_scales[g][:, r * P:(r + 1) * P],
-                            rhs=w_codes[g][h][:, c0:c0 + wd].bitcast(FP8X4),
-                            rhs_scale=w_scales[g][h][:, c0:c0 + wd],
-                            start=(s == 0), stop=(s == len(steps) - 1))
+            held[bank] = psum.tile([P, per_bank, wd], F32, name="sum%d_%d" % (c0, u), tag="bank%d" % bank)
+            for v in range(per_bank):
+                for g in range(PASSES):
+                    for h in range(2):
+                        product(held[bank][:, v, :], u * per_bank + v, g, h, c0, wd)
 
-        def drain(c, u):
-            c0, wd = CHUNKS[c]
+        def drain_bank(c0, wd, bank, u):
             per_bank = 512 // wd
+            k, o = span(Y_TILES, c0, wd)
             nc.vector.tensor_tensor(
-                out=y32[c][:, u * per_bank:(u + 1) * per_bank, :], in0=acc[(c, u)][:],
-                in1=bias[:, c0:c0 + wd].unsqueeze(1).to_broadcast([P, per_bank, wd]), op=ALU.add)
+                out=y32[k][:, u * per_bank:(u + 1) * per_bank, o:o + wd], in0=held[bank][:],
+                in1=bias[:, c0 - BIAS0:c0 - BIAS0 + wd].unsqueeze(1).to_broadcast([P, per_bank, wd]), op=ALU.add)
 
-        def store_y(c):
-            c0, wd = CHUNKS[c]
-            nc.sync.dma_start(out=out_rows[:, :, c0:c0 + wd], in_=y32[c][:])
+        def mm_rows(c0, wd, bank, g, h):
+            for r in range(PACK):
+                if g == 0 and h == 0:
+                    held[bank + r] = psum.tile([P, wd], F32, name="sum_r%d_%d" % (c0, r), tag="bank%d" % (bank + r))
+                product(held[bank + r][:], r, g, h, c0, wd)
 
-        def cast_y(c):
-            src = y32[c][:].rearrange("p r (c i) -> p c r i", i=2)
-            nc.scalar.copy(out=paired(y_bf[c]), in_=src)
+        def drain_rows(c0, wd, bank):
+            k, o = span(Y_TILES, c0, wd)
+            for r in range(PACK):
+                nc.vector.tensor_tensor(out=y32[k][:, r, o:o + wd], in0=held[bank + r][:],
+                                        in1=bias[:, c0 - BIAS0:c0 - BIAS0 + wd], op=ALU.add)
 
-        def quant_y(c):
-            c0, wd = CHUNKS[c]
-            nc.vector.quantize_mx(out=y_codes[c][:].bitcast(FP8X4), scales=y_scales[:, c0:c0 + wd], in_=y_bf[c][:])
+        def store_y(c0, wd):
+            k, o = span(Y_TILES, c0, wd)
+            nc.sync.dma_start(out=out_rows[:, :, c0:c0 + wd], in_=y32[k][:])
 
-        def store_words(c, eng):
-            c0, wd = CHUNKS[c]
-            eng.dma_start(out=out_words[:, c0:c0 + wd], in_=y_codes[c][:].bitcast(I32))
+        def cast_y(c0, wd):
+            k, o = span(Y_TILES, c0, wd)
+            kp, op = span(PLANES, c0, wd)
+            src = y32[k][:, :, o:o + wd].rearrange("p r (c i) -> p c r i", i=2)
+            nc.scalar.copy(out=paired(y_bf[kp][:, PACK * op:PACK * (op + wd)]), in_=src)
 
-        def store_scales(c0, c1, engs):
+        def quant_y(c0, wd):
+            k, o = span(PLANES, c0, wd)
+            nc.vector.quantize_mx(out=y_codes[k][:].bitcast(FP8X4), scales=y_scales[:, c0:c0 + wd], in_=y_bf[k][:])
+
+        def store_words(c0, wd, eng):
+            k, o = span(PLANES, c0, wd)
+            eng.dma_start(out=out_words[:, c0:c0 + wd], in_=y_codes[k][:].bitcast(I32))
+
+        def store_scales(c0, c1, two):
             for q in range(4):
-                engs[q % len(engs)].dma_start(
-                    out=out_scales[4 * q:4 * q + 4, c0 // 4:c1 // 4],
-                    in_=y_scales[32 * q:32 * q + 4, c0:c1].bitcast(I32))
+                eng = nc.scalar if two and q % 2 else nc.sync
+                eng.dma_start(out=out_scales[4 * q:4 * q + 4, c0 // 4:c1 // 4],
+                              in_=y_scales[32 * q:32 * q + 4, c0:c1].bitcast(I32))
 
-        def spread_bias(u):
-            spread = psum.tile([P, 4, P], F32, name="spread%d" % u, tag="bank%d" % (5 + u))
+        def bias_columns(bank):
+            b_turned = psum.tile([P, P], F32, name="b_turned", tag="bank%d" % bank)
+            nc.tensor.transpose(b_turned[:], b_rows[:], ident[:])
+            nc.scalar.copy(out=b_col[:], in_=b_turned[:, 0:B_COLS])
+
+        def spread(blk, bank):
+            held[bank] = psum.tile([P, 4, P], F32, name="spread%d" % blk, tag="bank%d" % bank)
             for v in range(4):
-                col = 4 * u + v
-                nc.tensor.transpose(spread[:, v, :], b_col[:, col:col + 1].to_broadcast([P, P]), ident[:])
-            acc[("b", u)] = spread
+                col = 4 * blk + v
+                nc.tensor.transpose(held[bank][:, v, :], b_col[:, col:col + 1].to_broadcast([P, P]), ident[:])
 
-        def copy_bias(u):
-            dst = bias[:].rearrange("q (p c) -> q p c", c=B_COLS)[:, :, 4 * u:4 * u + 4]
-            nc.scalar.copy(out=dst, in_=acc[("b", u)][:].rearrange("q v p -> q p v"))
+        def copy_bias(blk, bank):
+            nc.scalar.copy(out=bias[:, 512 * blk - BIAS0:512 * (blk + 1) - BIAS0], in_=held[bank][:].rearrange("q v p -> q (v p)"))
 
-        load_w(0)
-        load_w(1)
-        nc.sync.dma_start(out=b_col[:], in_=b.rearrange("(p c) -> p c", c=B_COLS))
-        for i in (2, 3, 4):
-            load_w(i)
-        load_x(0)
-        load_w(5)
-        load_x(1)
-        for i in (6, 7, 8):
-            load_w(i)
+        nc.gpsimd.memset(b_rows[:], 0.0)
         make_identity(nc, ident[:])
-        for u in range(3):
-            spread_bias(u)
-
-        def extras_s(i):
-            if i == 2:
-                copy_bias(0)
-            if i == 3:
-                copy_bias(1)
-                copy_bias(2)
-            if i == 4:
-                cast_x(0, 0)
-                cast_x(0, 1)
-            if i == 6:
-                cast_x(1, 0)
-                cast_x(1, 1)
-
-        def finish(c):
-            for u in range(banks_of(c)):
-                drain(c, u)
-            store_y(c)
-
-        def planes(c):
-            quant_y(c)
-            store_words(c, nc.sync)
-
-        n = len(PIECES)
+        load_w(0)
+        load_b()
+        load_w(1)
+        load_w(2)
+        load_w(3)
+        load_w(4)
+        load_w(5)
+        load_w(6)
+        load_x(0)
+        load_w(7)
+        load_x(1)
+        load_w(8)
+        load_w(9)
+        load_w(10)
+        load_w(11)
+        load_w(12)
+        load_w(13)
         upper(0)
         upper(1)
         mask(0)
-        quant_w(0, 0)
-        for i in range(n):
-            if i + 2 < n:
-                upper(i + 2)
-                extras_s(i + 2)
-            lower(i)
-            if i == 4:
-                quant_x(0)
-            if i == 6:
-                quant_x(1)
-                matmuls(0)
-                matmuls(1)
-            if i + 1 < n:
-                mask(i + 1)
-            else:
-                planes(4)
-            quant_w(i, 1)
-            if i + 1 < n:
-                quant_w(i + 1, 0)
-            if i == 7:
-                matmuls(2)
-                finish(0)
-                cast_y(0)
-            if i == 8:
-                matmuls(3)
-                finish(1)
-                cast_y(1)
-                planes(0)
-            if i == 9:
-                finish(2)
-                cast_y(2)
-                planes(1)
-            if i == 10:
-                matmuls(4)
-                finish(3)
-                cast_y(3)
-                planes(2)
-            if i == 11:
-                planes(3)
-                store_scales(0, 1024, [nc.sync])
-                finish(4)
-                cast_y(4)
-            if i == 12:
-                matmuls(5)
-        matmuls(6)
-        finish(5)
-        cast_y(5)
-        finish(6)
-        cast_y(6)
-        planes(5)
-        quant_y(6)
-        store_words(6, nc.scalar)
-        store_scales(1024, M, [nc.sync, nc.scalar])
+        bias_columns(7)
+        spread(1, 5)
+        spread(2, 6)
+        upper(2)
+        lower(0)
+        mask(1)
+        quant_both(0)
+        upper(3)
+        lower(1)
+        mask(2)
+        quant_both(1)
+        copy_bias(1, 5)
+        upper(4)
+        lower(2)
+        mask(3)
+        quant_both(2)
+        copy_bias(2, 6)
+        upper(5)
+        lower(3)
+        mask(4)
+        quant_both(3)
+        upper(6)
+        lower(4)
+        mask(5)
+        quant_both(4)
+        cast_x(0, 0)
+        cast_x(0, 1)
+        upper(7)
+        lower(5)
+        mask(6)
+        quant_both(5)
+        cast_x(1, 0)
+        cast_x(1, 1)
+        lower(6)
+        quant_x(0)
+        quant_both(6)
+        mask(7)
+        mm_turned(0, 0, 0)
+        mm_turned(128, 0, 1)
+        mm_turned(256, 0, 2)
+        mm_turned(384, 0, 3)
+        upper(8)
+        upper(9)
+        upper(10)
+        lower(7)
+        quant_x(1)
+        quant_both(7)
+        mask(8)
+        mm_turned(0, 1, 0)
+        mm_turned(128, 1, 1)
+        mm_bank(512, 256, 4, 0)
+        mm_bank(512, 256, 5, 1)
+        mm_turned(256, 1, 2)
+        mm_turned(384, 1, 3)
+        lower(8)
+        mask(9)
+        quant_both(8)
+        drain_turned(0, 0)
+        drain_turned(128, 1)
+        upper(11)
+        turn(0, 0)
+        turn(128, 1)
+        lower(9)
+        mask(10)
+        quant_both(9)
+        drain_bank(512, 256, 4, 0)
+        drain_bank(512, 256, 5, 1)
+        store_y(512, 256)
+        mm_bank(768, 256, 6, 0)
+        mm_bank(768, 256, 7, 1)
+        drain_turned(256, 2)
+        drain_turned(384, 3)
+        copy_turned(0, 0)
+        copy_turned(128, 1)
+        store_y(0, 256)
+        turn(256, 2)
+        turn(384, 3)
+        upper(12)
+        lower(10)
+        mask(11)
+        quant_both(10)
+        copy_turned(256, 2)
+        copy_turned(384, 3)
+        drain_bank(768, 256, 6, 0)
+        drain_bank(768, 256, 7, 1)
+        store_y(768, 256)
+        store_y(256, 256)
+        upper(13)
+        upper(14)
+        cast_y(512, 256)
+        cast_y(768, 256)
+        lower(11)
+        mask(12)
+        quant_both(11)
+        mm_bank(1024, 256, 4, 0)
+        mm_bank(1024, 256, 5, 1)
+        cast_y(0, 256)
+        cast_y(256, 256)
+        lower(12)
+        mask(13)
+        quant_y(512, 512)
+        store_words(512, 512, nc.sync)
+        quant_both(12)
+        mm_rows(1408, 128, 0, 0, 0)
+        mm_rows(1408, 128, 0, 0, 1)
+        drain_bank(1024, 256, 4, 0)
+        drain_bank(1024, 256, 5, 1)
+        store_y(1024, 256)
+        cast_y(1024, 256)
+        lower(13)
+        mask(14)
+        quant_both(13)
+        mm_bank(1280, 128, 6, 0)
+        quant_part(14, 0)
+        mm_rows(1408, 128, 0, 1, 0)
+        quant_y(0, 512)
+        store_words(0, 512, nc.sync)
+        store_scales(0, 1024, False)
+        lower(14)
+        drain_bank(1280, 128, 6, 0)
+        store_y(1280, 128)
+        cast_y(1280, 128)
+        quant_part(14, 1)
+        mm_rows(1408, 128, 0, 1, 1)
+        quant_y(1024, 256)
+        store_words(1024, 256, nc.sync)
+        drain_rows(1408, 128, 0)
+        store_y(1408, 128)
+        cast_y(1408, 128)
+        quant_y(1280, 128)
+        store_words(1280, 128, nc.sync)
+        quant_y(1408, 128)
+        store_words(1408, 128, nc.scalar)
+        store_scales(1024, 1536, True)

@@ -26,7 +26,8 @@ BIAS0 = 512
 W_LOADS = [(0, 0, 128), (0, 128, 128), (0, 256, 128), (0, 384, 128), (1, 0, 256), (1, 256, 256), (0, 512, 256), (1, 512, 256), (0, 768, 256), (1, 768, 256), (0, 1024, 256), (1, 1024, 256), (0, 1280, 256), (1, 1280, 256)]
 PIECES = [(0, 0, 128), (0, 128, 128), (0, 256, 128), (0, 384, 128), (1, 0, 256), (1, 256, 256), (0, 512, 256), (1, 512, 256), (0, 768, 256), (1, 768, 256), (0, 1024, 256), (1, 1024, 256), (0, 1280, 256), (1, 1280, 128), (1, 1408, 128)]
 Y_TILES = [(0, 256), (256, 256), (512, 256), (768, 256), (1024, 256), (1280, 128), (1408, 128)]
-PLANES = [(0, 512), (512, 512), (1024, 256), (1280, 128), (1408, 128)]
+WORD_TILES = [(0, 1024), (1024, 512)]
+PLANES = [(0, 512), (512, 512), (1024, 256), (1280, 256)]
 
 
 def tile_mix_hilo_tm_pl_bias_kernel(tc, w, x, b, out_0, out_1, out_2):
@@ -54,7 +55,7 @@ def tile_mix_hilo_tm_pl_bias_kernel(tc, w, x, b, out_0, out_1, out_2):
         w_scales = [keep.tile([P, 2, wd], U8, name="w_scales%d" % i, align_bytes=64) for i, (g, c0, wd) in enumerate(PIECES)]
         y32 = [keep.tile([P, PACK, wd], F32, name="y32_%d" % i) for i, (c0, wd) in enumerate(Y_TILES)]
         y_bf = [keep.tile([P, PACK * wd], BF16, name="y_bf%d" % i, align_bytes=64) for i, (c0, wd) in enumerate(PLANES)]
-        y_codes = [keep.tile([P, wd], U32, name="y_codes%d" % i, align_bytes=64) for i, (c0, wd) in enumerate(PLANES)]
+        y_codes = [keep.tile([P, wd], U32, name="y_codes%d" % i, align_bytes=64) for i, (c0, wd) in enumerate(WORD_TILES)]
         y_scales = keep.tile([P, M], U8, name="y_scales", align_bytes=64)
         held = {}
 
@@ -85,6 +86,12 @@ def tile_mix_hilo_tm_pl_bias_kernel(tc, w, x, b, out_0, out_1, out_2):
             halves = w_raw[k][:].bitcast(BF16)[:, :, 2 * o:2 * (o + wd)].rearrange("p j (c i h) -> p c j i h", i=2, h=2)
             nc.scalar.copy(out=paired(w_bf[i][:, 0, :]), in_=halves[:, :, :, :, 1])
 
+        def upper_v(i):
+            g, c0, wd = PIECES[i]
+            k, o = holder(W_LOADS, g, c0, wd)
+            halves = w_raw[k][:].bitcast(BF16)[:, :, 2 * o:2 * (o + wd)].rearrange("p j (c i h) -> p c j i h", i=2, h=2)
+            nc.vector.tensor_copy(out=paired(w_bf[i][:, 0, :]), in_=halves[:, :, :, :, 1])
+
         def mask(i):
             words = w_bf[i][:, 0, :].bitcast(I32)
             nc.vector.tensor_scalar(out=words, in0=words, scalar1=HI_MASK_PAIR, scalar2=None, op0=ALU.bitwise_and)
@@ -107,6 +114,11 @@ def tile_mix_hilo_tm_pl_bias_kernel(tc, w, x, b, out_0, out_1, out_2):
             dst = x_bf[g][:].rearrange("p (u v m j) -> p u m j v", u=2, v=2, j=PACK)
             src = x_raw[g][:].rearrange("p j (m u v) -> p u m j v", u=2, v=2)
             nc.scalar.copy(out=dst[:, half], in_=src[:, half])
+
+        def cast_xv(g, half):
+            dst = x_bf[g][:].rearrange("p (u v m j) -> p u m j v", u=2, v=2, j=PACK)
+            src = x_raw[g][:].rearrange("p j (m u v) -> p u m j v", u=2, v=2)
+            nc.vector.tensor_copy(out=dst[:, half], in_=src[:, half])
 
         def quant_x(g):
             nc.vector.quantize_mx(out=x_codes[g][:].bitcast(FP8X4), scales=x_scales[g][:], in_=x_bf[g][:])
@@ -188,10 +200,11 @@ def tile_mix_hilo_tm_pl_bias_kernel(tc, w, x, b, out_0, out_1, out_2):
 
         def quant_y(c0, wd):
             k, o = span(PLANES, c0, wd)
-            nc.vector.quantize_mx(out=y_codes[k][:].bitcast(FP8X4), scales=y_scales[:, c0:c0 + wd], in_=y_bf[k][:])
+            kw, ow = span(WORD_TILES, c0, wd)
+            nc.vector.quantize_mx(out=y_codes[kw][:, ow:ow + wd].bitcast(FP8X4), scales=y_scales[:, c0:c0 + wd], in_=y_bf[k][:])
 
         def store_words(c0, wd, eng):
-            k, o = span(PLANES, c0, wd)
+            k, o = span(WORD_TILES, c0, wd)
             eng.dma_start(out=out_words[:, c0:c0 + wd], in_=y_codes[k][:].bitcast(I32))
 
         def store_scales(c0, c1, two):
@@ -214,12 +227,12 @@ def tile_mix_hilo_tm_pl_bias_kernel(tc, w, x, b, out_0, out_1, out_2):
         def copy_bias(blk, bank):
             nc.scalar.copy(out=bias[:, 512 * blk - BIAS0:512 * (blk + 1) - BIAS0], in_=held[bank][:].rearrange("q v p -> q (v p)"))
 
-        nc.gpsimd.memset(b_rows[:], 0.0)
+        nc.vector.memset(b_rows[:], 0.0)
         make_identity(nc, ident[:])
         load_w(0)
-        load_b()
         load_w(1)
         load_w(2)
+        load_b()
         load_w(3)
         load_w(4)
         load_w(5)
@@ -233,140 +246,138 @@ def tile_mix_hilo_tm_pl_bias_kernel(tc, w, x, b, out_0, out_1, out_2):
         load_w(11)
         load_w(12)
         load_w(13)
-        upper(0)
-        upper(1)
+        upper_v(0)
         mask(0)
-        bias_columns(7)
-        spread(1, 5)
-        spread(2, 6)
-        upper(2)
+        upper(1)
         lower(0)
         mask(1)
         quant_both(0)
-        upper(3)
+        upper(2)
         lower(1)
         mask(2)
         quant_both(1)
-        copy_bias(1, 5)
-        upper(4)
+        upper(3)
         lower(2)
         mask(3)
         quant_both(2)
-        copy_bias(2, 6)
-        upper(5)
+        bias_columns(7)
+        spread(1, 5)
+        spread(2, 6)
+        upper(4)
         lower(3)
         mask(4)
         quant_both(3)
-        upper(6)
+        upper(5)
+        copy_bias(1, 5)
         lower(4)
         mask(5)
         quant_both(4)
-        cast_x(0, 0)
-        cast_x(0, 1)
-        upper(7)
+        upper(6)
+        copy_bias(2, 6)
         lower(5)
         mask(6)
         quant_both(5)
-        cast_x(1, 0)
-        cast_x(1, 1)
+        cast_x(0, 0)
+        cast_x(0, 1)
+        upper(7)
         lower(6)
         quant_x(0)
         quant_both(6)
-        mask(7)
         mm_turned(0, 0, 0)
         mm_turned(128, 0, 1)
         mm_turned(256, 0, 2)
         mm_turned(384, 0, 3)
+        mask(7)
+        cast_x(1, 0)
+        cast_xv(1, 1)
         upper(8)
-        upper(9)
-        upper(10)
         lower(7)
         quant_x(1)
-        quant_both(7)
         mask(8)
+        quant_both(7)
         mm_turned(0, 1, 0)
         mm_turned(128, 1, 1)
-        mm_bank(512, 256, 4, 0)
-        mm_bank(512, 256, 5, 1)
         mm_turned(256, 1, 2)
         mm_turned(384, 1, 3)
+        mm_bank(512, 256, 4, 0)
+        mm_bank(512, 256, 5, 1)
+        upper(9)
+        upper(10)
         lower(8)
         mask(9)
         quant_both(8)
+        mask(10)
         drain_turned(0, 0)
-        drain_turned(128, 1)
         upper(11)
+        drain_turned(128, 1)
         turn(0, 0)
         turn(128, 1)
         lower(9)
-        mask(10)
-        quant_both(9)
+        mask(11)
         drain_bank(512, 256, 4, 0)
-        drain_bank(512, 256, 5, 1)
-        store_y(512, 256)
+        quant_both(9)
         mm_bank(768, 256, 6, 0)
         mm_bank(768, 256, 7, 1)
+        upper(12)
         drain_turned(256, 2)
         drain_turned(384, 3)
-        copy_turned(0, 0)
-        copy_turned(128, 1)
-        store_y(0, 256)
         turn(256, 2)
         turn(384, 3)
-        upper(12)
+        copy_turned(0, 0)
+        copy_turned(128, 1)
         lower(10)
-        mask(11)
+        mask(12)
+        drain_bank(512, 256, 5, 1)
+        store_y(512, 256)
+        store_y(0, 256)
         quant_both(10)
-        copy_turned(256, 2)
-        copy_turned(384, 3)
-        drain_bank(768, 256, 6, 0)
-        drain_bank(768, 256, 7, 1)
-        store_y(768, 256)
-        store_y(256, 256)
         upper(13)
         upper(14)
+        copy_turned(256, 2)
+        copy_turned(384, 3)
+        store_y(256, 256)
         cast_y(512, 256)
-        cast_y(768, 256)
         lower(11)
-        mask(12)
+        mask(13)
+        drain_bank(768, 256, 6, 0)
         quant_both(11)
         mm_bank(1024, 256, 4, 0)
         mm_bank(1024, 256, 5, 1)
+        drain_bank(768, 256, 7, 1)
+        store_y(768, 256)
+        cast_y(768, 256)
         cast_y(0, 256)
         cast_y(256, 256)
         lower(12)
-        mask(13)
-        quant_y(512, 512)
-        store_words(512, 512, nc.sync)
+        mask(14)
         quant_both(12)
         mm_rows(1408, 128, 0, 0, 0)
         mm_rows(1408, 128, 0, 0, 1)
         drain_bank(1024, 256, 4, 0)
+        lower(13)
+        quant_part(14, 0)
         drain_bank(1024, 256, 5, 1)
         store_y(1024, 256)
         cast_y(1024, 256)
-        lower(13)
-        mask(14)
-        quant_both(13)
-        mm_bank(1280, 128, 6, 0)
-        quant_part(14, 0)
         mm_rows(1408, 128, 0, 1, 0)
-        quant_y(0, 512)
-        store_words(0, 512, nc.sync)
-        store_scales(0, 1024, False)
+        mm_rows(1280, 128, 4, 0, 0)
+        mm_rows(1280, 128, 4, 0, 1)
+        quant_y(512, 512)
+        quant_both(13)
+        mm_rows(1280, 128, 4, 1, 0)
+        mm_rows(1280, 128, 4, 1, 1)
         lower(14)
-        drain_bank(1280, 128, 6, 0)
-        store_y(1280, 128)
-        cast_y(1280, 128)
+        quant_y(0, 512)
+        store_words(0, 1024, nc.sync)
         quant_part(14, 1)
         mm_rows(1408, 128, 0, 1, 1)
-        quant_y(1024, 256)
-        store_words(1024, 256, nc.sync)
+        drain_rows(1280, 128, 4)
+        store_y(1280, 128)
+        cast_y(1280, 128)
         drain_rows(1408, 128, 0)
         store_y(1408, 128)
         cast_y(1408, 128)
-        quant_y(1280, 128)
-        store_words(1280, 128, nc.sync)
-        quant_y(1408, 128)
-        store_words(1408, 128, nc.scalar)
-        store_scales(1024, 1536, True)
+        quant_y(1024, 256)
+        quant_y(1280, 256)
+        store_words(1024, 512, nc.scalar)
+        store_scales(0, 1536, True)

@@ -26,7 +26,8 @@ BIAS0 = 512
 W_LOADS = [(0, 0, 128), (0, 128, 128), (0, 256, 128), (0, 384, 128), (1, 0, 256), (1, 256, 256), (0, 512, 256), (1, 512, 256), (0, 768, 256), (1, 768, 256), (0, 1024, 256), (1, 1024, 256), (0, 1280, 256), (1, 1280, 256)]
 PIECES = [(0, 0, 128), (0, 128, 128), (0, 256, 128), (0, 384, 128), (1, 0, 256), (1, 256, 256), (0, 512, 256), (1, 512, 256), (0, 768, 256), (1, 768, 256), (0, 1024, 256), (1, 1024, 256), (0, 1280, 256), (1, 1280, 128), (1, 1408, 128)]
 Y_TILES = [(0, 256), (256, 256), (512, 256), (768, 256), (1024, 256), (1280, 128), (1408, 128)]
-WORD_TILES = [(0, 1024), (1024, 512)]
+WORD_TILES = [(0, 512), (512, 512), (1024, 512)]
+GP_COLS = {11: 80, 12: 80, 14: 80}
 PLANES = [(0, 512), (512, 512), (1024, 256), (1280, 256)]
 
 
@@ -96,11 +97,18 @@ def tile_mix_hilo_tm_pl_bias_kernel(tc, w, x, b, out_0, out_1, out_2):
             words = w_bf[i][:, 0, :].bitcast(I32)
             nc.vector.tensor_scalar(out=words, in0=words, scalar1=HI_MASK_PAIR, scalar2=None, op0=ALU.bitwise_and)
 
-        def lower(i):
+        def lower_cols(eng, i, a, z):
             g, c0, wd = PIECES[i]
             k, o = holder(W_LOADS, g, c0, wd)
-            src = w_raw[k][:, :, o:o + wd].rearrange("p j (c i) -> p c j i", i=2)
-            nc.vector.tensor_tensor(out=paired(w_bf[i][:, 1, :]), in0=src, in1=paired(w_bf[i][:, 0, :]), op=ALU.subtract)
+            src = w_raw[k][:, :, o + a:o + z].rearrange("p j (c i) -> p c j i", i=2)
+            eng.tensor_tensor(out=paired(w_bf[i][:, 1, PACK * a:PACK * z]), in0=src,
+                              in1=paired(w_bf[i][:, 0, PACK * a:PACK * z]), op=ALU.subtract)
+
+        def lower(i):
+            lower_cols(nc.vector, i, 0, PIECES[i][2] - GP_COLS.get(i, 0))
+
+        def lower_g(i):
+            lower_cols(nc.gpsimd, i, PIECES[i][2] - GP_COLS[i], PIECES[i][2])
 
         def quant_part(i, h):
             nc.vector.quantize_mx(out=w_codes[i][:, h, :].bitcast(FP8X4), scales=w_scales[i][:, h, :], in_=w_bf[i][:, h, :])
@@ -314,10 +322,13 @@ def tile_mix_hilo_tm_pl_bias_kernel(tc, w, x, b, out_0, out_1, out_2):
         turn(128, 1)
         lower(9)
         mask(11)
-        drain_bank(512, 256, 4, 0)
         quant_both(9)
+        lower_g(11)
         mm_bank(768, 256, 6, 0)
         mm_bank(768, 256, 7, 1)
+        drain_bank(512, 256, 4, 0)
+        drain_bank(512, 256, 5, 1)
+        store_y(512, 256)
         upper(12)
         drain_turned(256, 2)
         drain_turned(384, 3)
@@ -325,56 +336,57 @@ def tile_mix_hilo_tm_pl_bias_kernel(tc, w, x, b, out_0, out_1, out_2):
         turn(384, 3)
         copy_turned(0, 0)
         copy_turned(128, 1)
+        store_y(0, 256)
         lower(10)
         mask(12)
-        drain_bank(512, 256, 5, 1)
-        store_y(512, 256)
-        store_y(0, 256)
         quant_both(10)
+        lower_g(12)
+        drain_bank(768, 256, 6, 0)
+        drain_bank(768, 256, 7, 1)
+        store_y(768, 256)
         upper(13)
         upper(14)
+        cast_y(512, 256)
+        cast_y(768, 256)
         copy_turned(256, 2)
         copy_turned(384, 3)
         store_y(256, 256)
-        cast_y(512, 256)
+        cast_y(0, 256)
+        cast_y(256, 256)
         lower(11)
         mask(13)
-        drain_bank(768, 256, 6, 0)
         quant_both(11)
         mm_bank(1024, 256, 4, 0)
         mm_bank(1024, 256, 5, 1)
-        drain_bank(768, 256, 7, 1)
-        store_y(768, 256)
-        cast_y(768, 256)
-        cast_y(0, 256)
-        cast_y(256, 256)
         lower(12)
-        mask(14)
+        quant_y(512, 512)
+        store_words(512, 512, nc.sync)
         quant_both(12)
-        mm_rows(1408, 128, 0, 0, 0)
-        mm_rows(1408, 128, 0, 0, 1)
-        drain_bank(1024, 256, 4, 0)
+        mm_rows(1280, 128, 0, 0, 0)
+        mm_rows(1280, 128, 0, 0, 1)
         lower(13)
-        quant_part(14, 0)
+        mask(14)
+        quant_both(13)
+        lower_g(14)
+        mm_rows(1280, 128, 0, 1, 0)
+        mm_rows(1280, 128, 0, 1, 1)
+        drain_bank(1024, 256, 4, 0)
         drain_bank(1024, 256, 5, 1)
         store_y(1024, 256)
         cast_y(1024, 256)
-        mm_rows(1408, 128, 0, 1, 0)
-        mm_rows(1280, 128, 4, 0, 0)
-        mm_rows(1280, 128, 4, 0, 1)
-        quant_y(512, 512)
-        quant_both(13)
-        mm_rows(1280, 128, 4, 1, 0)
-        mm_rows(1280, 128, 4, 1, 1)
+        mm_rows(1408, 128, 4, 0, 0)
+        mm_rows(1408, 128, 4, 0, 1)
         lower(14)
+        quant_part(14, 0)
+        mm_rows(1408, 128, 4, 1, 0)
         quant_y(0, 512)
-        store_words(0, 1024, nc.sync)
+        store_words(0, 512, nc.sync)
         quant_part(14, 1)
-        mm_rows(1408, 128, 0, 1, 1)
-        drain_rows(1280, 128, 4)
+        mm_rows(1408, 128, 4, 1, 1)
+        drain_rows(1280, 128, 0)
         store_y(1280, 128)
         cast_y(1280, 128)
-        drain_rows(1408, 128, 0)
+        drain_rows(1408, 128, 4)
         store_y(1408, 128)
         cast_y(1408, 128)
         quant_y(1024, 256)

@@ -19,16 +19,34 @@ P = 128
 PACK = 4
 K_PASS = P * PACK
 PASSES = K // K_PASS
+BANK = 512
+HI, LO = 0, 1
 HI_MASK_PAIR = 0xFFF0FFF0 - (1 << 32)
-B_COLS = M // P
-BIAS0 = 512
+B_ROWS = M // P
+TURNED_COLS = 512
 
-W_LOADS = [(0, 0, 128), (0, 128, 128), (0, 256, 128), (0, 384, 128), (1, 0, 256), (1, 256, 256), (0, 512, 256), (1, 512, 256), (0, 768, 256), (1, 768, 256), (0, 1024, 256), (1, 1024, 256), (0, 1280, 256), (1, 1280, 256)]
-PIECES = [(0, 0, 128), (0, 128, 128), (0, 256, 128), (0, 384, 128), (1, 0, 256), (1, 256, 256), (0, 512, 256), (1, 512, 256), (0, 768, 256), (1, 768, 256), (0, 1024, 256), (1, 1024, 256), (0, 1280, 256), (1, 1280, 128), (1, 1408, 128)]
-Y_TILES = [(0, 256), (256, 256), (512, 256), (768, 256), (1024, 256), (1280, 128), (1408, 128)]
-WORD_TILES = [(0, 512), (512, 512), (1024, 512)]
-GP_COLS = {11: 80, 12: 80, 14: 80}
-PLANES = [(0, 512), (512, 512), (1024, 256), (1280, 256)]
+W_LOADS = [(0, 0, 128), (0, 128, 128), (0, 256, 256), (1, 0, 256), (1, 256, 256)] + [
+    (g, c0, 256) for c0 in range(TURNED_COLS, M, 256) for g in range(PASSES)
+]
+PIECES = W_LOADS[:2] + [(0, 256, 128), (0, 384, 128)] + W_LOADS[3:-1] + [(1, 1280, 128), (1, 1408, 128)]
+LAST = len(PIECES) - 1
+GPSIMD_COLS = {11: 80, 12: 80, LAST: 80}
+Y_TILES = [(c0, 256) for c0 in range(0, 1280, 256)] + [(1280, 128), (1408, 128)]
+Y_QUANTS = [(0, 512), (512, 512), (1024, 256), (1280, 128), (1408, 128)]
+WORD_TILES = [(0, 512), (512, 512), (1024, 384), (1408, 128)]
+
+
+def find(ranges, key):
+    c0, wd = key[-2:]
+    return [
+        (i, c0 - entry[-2])
+        for i, entry in enumerate(ranges)
+        if entry[:-2] == key[:-2] and entry[-2] <= c0 and c0 + wd <= entry[-2] + entry[-1]
+    ][0]
+
+
+def paired(packed):
+    return packed.rearrange("p (c i j) -> p c j i", i=2, j=PACK)
 
 
 def tile_mix_hilo_tm_pl_bias_kernel(tc, w, x, b, out_0, out_1, out_2):
@@ -44,8 +62,8 @@ def tile_mix_hilo_tm_pl_bias_kernel(tc, w, x, b, out_0, out_1, out_2):
 
         ident = keep.tile([P, P], F32, name="ident")
         b_rows = keep.tile([P, P], F32, name="b_rows")
-        b_col = keep.tile([P, B_COLS], F32, name="b_col")
-        bias = keep.tile([P, M - BIAS0], F32, name="bias")
+        b_col = keep.tile([P, B_ROWS], F32, name="b_col")
+        bias = keep.tile([P, M - TURNED_COLS], F32, name="bias")
         w_raw = [keep.tile([P, PACK, wd], F32, name="w_raw%d" % i) for i, (g, c0, wd) in enumerate(W_LOADS)]
         x_raw = [keep.tile([P, PACK, T], F32, name="x_raw%d" % g) for g in range(PASSES)]
         x_bf = [keep.tile([P, PACK * T], BF16, name="x_bf%d" % g, align_bytes=64) for g in range(PASSES)]
@@ -55,16 +73,22 @@ def tile_mix_hilo_tm_pl_bias_kernel(tc, w, x, b, out_0, out_1, out_2):
         w_codes = [keep.tile([P, 2, wd], U32, name="w_codes%d" % i, align_bytes=64) for i, (g, c0, wd) in enumerate(PIECES)]
         w_scales = [keep.tile([P, 2, wd], U8, name="w_scales%d" % i, align_bytes=64) for i, (g, c0, wd) in enumerate(PIECES)]
         y32 = [keep.tile([P, PACK, wd], F32, name="y32_%d" % i) for i, (c0, wd) in enumerate(Y_TILES)]
-        y_bf = [keep.tile([P, PACK * wd], BF16, name="y_bf%d" % i, align_bytes=64) for i, (c0, wd) in enumerate(PLANES)]
+        y_bf = [keep.tile([P, PACK * wd], BF16, name="y_bf%d" % i, align_bytes=64) for i, (c0, wd) in enumerate(Y_QUANTS)]
         y_codes = [keep.tile([P, wd], U32, name="y_codes%d" % i, align_bytes=64) for i, (c0, wd) in enumerate(WORD_TILES)]
         y_scales = keep.tile([P, M], U8, name="y_scales", align_bytes=64)
-        held = {}
+        in_bank = {}
+        y_t = {}
 
-        def holder(spans, g, c0, wd):
-            return [(k, c0 - s0) for k, (sg, s0, sw) in enumerate(spans) if sg == g and s0 <= c0 and c0 + wd <= s0 + sw][0]
+        def bank_tile(bank, shape, name):
+            in_bank[bank] = psum.tile(shape, F32, name=name, tag="bank%d" % bank)
+            return in_bank[bank]
 
-        def span(spans, c0, wd):
-            return [(k, c0 - s0) for k, (s0, sw) in enumerate(spans) if s0 <= c0 and c0 + wd <= s0 + sw][0]
+        def copy_on(eng, out, in_):
+            if eng is nc.scalar:
+                nc.scalar.copy(out=out, in_=in_)
+            else:
+                nc.vector.tensor_copy(out=out, in_=in_)
+
 
         def load_w(i):
             g, c0, wd = W_LOADS[i]
@@ -75,40 +99,27 @@ def tile_mix_hilo_tm_pl_bias_kernel(tc, w, x, b, out_0, out_1, out_2):
             rows = x[g * K_PASS:(g + 1) * K_PASS, :]
             nc.sync.dma_start(out=x_raw[g][:], in_=rows.rearrange("(p j) t -> p j t", j=PACK))
 
-        def load_b():
-            nc.sync.dma_start(out=b_rows[0:B_COLS, :], in_=b.rearrange("(c p) -> c p", p=P))
-
-        def paired(ap):
-            return ap.rearrange("p (c i j) -> p c j i", i=2, j=PACK)
-
-        def upper(i):
-            g, c0, wd = PIECES[i]
-            k, o = holder(W_LOADS, g, c0, wd)
-            halves = w_raw[k][:].bitcast(BF16)[:, :, 2 * o:2 * (o + wd)].rearrange("p j (c i h) -> p c j i h", i=2, h=2)
-            nc.scalar.copy(out=paired(w_bf[i][:, 0, :]), in_=halves[:, :, :, :, 1])
-
-        def upper_v(i):
-            g, c0, wd = PIECES[i]
-            k, o = holder(W_LOADS, g, c0, wd)
-            halves = w_raw[k][:].bitcast(BF16)[:, :, 2 * o:2 * (o + wd)].rearrange("p j (c i h) -> p c j i h", i=2, h=2)
-            nc.vector.tensor_copy(out=paired(w_bf[i][:, 0, :]), in_=halves[:, :, :, :, 1])
+        def upper(i, eng=nc.scalar):
+            k, o = find(W_LOADS, PIECES[i])
+            halves = w_raw[k][:].bitcast(BF16)[:, :, 2 * o:2 * (o + PIECES[i][2])]
+            halves = halves.rearrange("p j (c i h) -> p c j i h", i=2, h=2)
+            copy_on(eng, paired(w_bf[i][:, HI, :]), halves[:, :, :, :, 1])
 
         def mask(i):
-            words = w_bf[i][:, 0, :].bitcast(I32)
+            words = w_bf[i][:, HI, :].bitcast(I32)
             nc.vector.tensor_scalar(out=words, in0=words, scalar1=HI_MASK_PAIR, scalar2=None, op0=ALU.bitwise_and)
 
-        def lower_cols(eng, i, a, z):
-            g, c0, wd = PIECES[i]
-            k, o = holder(W_LOADS, g, c0, wd)
-            src = w_raw[k][:, :, o + a:o + z].rearrange("p j (c i) -> p c j i", i=2)
-            eng.tensor_tensor(out=paired(w_bf[i][:, 1, PACK * a:PACK * z]), in0=src,
-                              in1=paired(w_bf[i][:, 0, PACK * a:PACK * z]), op=ALU.subtract)
+        def subtract(eng, i, first, end):
+            k, o = find(W_LOADS, PIECES[i])
+            src = w_raw[k][:, :, o + first:o + end].rearrange("p j (c i) -> p c j i", i=2)
+            eng.tensor_tensor(out=paired(w_bf[i][:, LO, PACK * first:PACK * end]), in0=src,
+                              in1=paired(w_bf[i][:, HI, PACK * first:PACK * end]), op=ALU.subtract)
 
         def lower(i):
-            lower_cols(nc.vector, i, 0, PIECES[i][2] - GP_COLS.get(i, 0))
+            subtract(nc.vector, i, 0, PIECES[i][2] - GPSIMD_COLS.get(i, 0))
 
-        def lower_g(i):
-            lower_cols(nc.gpsimd, i, PIECES[i][2] - GP_COLS[i], PIECES[i][2])
+        def lower_on_gpsimd(i):
+            subtract(nc.gpsimd, i, PIECES[i][2] - GPSIMD_COLS[i], PIECES[i][2])
 
         def quant_part(i, h):
             nc.vector.quantize_mx(out=w_codes[i][:, h, :].bitcast(FP8X4), scales=w_scales[i][:, h, :], in_=w_bf[i][:, h, :])
@@ -118,278 +129,258 @@ def tile_mix_hilo_tm_pl_bias_kernel(tc, w, x, b, out_0, out_1, out_2):
                                   scales=w_scales[i][:].rearrange("p h n -> p (h n)"),
                                   in_=w_bf[i][:].rearrange("p h n -> p (h n)"))
 
-        def cast_x(g, half):
+        def cast_x(g, half, eng=nc.scalar):
             dst = x_bf[g][:].rearrange("p (u v m j) -> p u m j v", u=2, v=2, j=PACK)
             src = x_raw[g][:].rearrange("p j (m u v) -> p u m j v", u=2, v=2)
-            nc.scalar.copy(out=dst[:, half], in_=src[:, half])
-
-        def cast_xv(g, half):
-            dst = x_bf[g][:].rearrange("p (u v m j) -> p u m j v", u=2, v=2, j=PACK)
-            src = x_raw[g][:].rearrange("p j (m u v) -> p u m j v", u=2, v=2)
-            nc.vector.tensor_copy(out=dst[:, half], in_=src[:, half])
+            copy_on(eng, dst[:, half], src[:, half])
 
         def quant_x(g):
             nc.vector.quantize_mx(out=x_codes[g][:].bitcast(FP8X4), scales=x_scales[g][:], in_=x_bf[g][:])
 
+
+        def load_b():
+            nc.sync.dma_start(out=b_rows[0:B_ROWS, :], in_=b.rearrange("(c p) -> c p", p=P))
+
+        def bias_columns(bank):
+            b_turned = bank_tile(bank, [P, P], "b_turned")
+            nc.tensor.transpose(b_turned[:], b_rows[:], ident[:])
+            nc.scalar.copy(out=b_col[:], in_=b_turned[:, 0:B_ROWS])
+
+        def spread_bias(c0, bank):
+            spread = bank_tile(bank, [P, BANK // P, P], "spread%d" % c0)
+            for v in range(BANK // P):
+                col = c0 // P + v
+                nc.tensor.transpose(spread[:, v, :], b_col[:, col:col + 1].to_broadcast([P, P]), ident[:])
+
+        def copy_bias(c0, bank):
+            nc.scalar.copy(out=bias[:, c0 - TURNED_COLS:c0 - TURNED_COLS + BANK],
+                           in_=in_bank[bank][:].rearrange("q v p -> q (v p)"))
+
+
+        def products_turned(c0, g):
+            k, o = find(PIECES, (g, c0, P))
+            if g == 0:
+                bank_tile(c0 // P, [P, T], "sum_t%d" % c0)
+            for h in (HI, LO):
+                nc.tensor.matmul_mx(
+                    out=in_bank[c0 // P][:],
+                    lhsT=w_codes[k][:, h, o:o + P].bitcast(FP8X4),
+                    lhsT_scale=w_scales[k][:, h, o:o + P],
+                    rhs=x_codes[g][:].bitcast(FP8X4),
+                    rhs_scale=x_scales[g][:],
+                    start=(g == 0 and h == HI), stop=(g == PASSES - 1 and h == LO))
+
+        def drain_turned(c0):
+            y_t[c0] = keep.tile([P, T], F32, name="y_t%d" % c0)
+            nc.scalar.activation(out=y_t[c0][:], in_=in_bank[c0 // P][:], func=ACT.Identity,
+                                 bias=b_col[:, c0 // P:c0 // P + 1], scale=1.0)
+
+        def turn(c0):
+            turned = bank_tile(c0 // P, [P, PACK, P], "turned%d" % c0)
+            for r in range(PACK):
+                nc.tensor.transpose(turned[:, r, :], y_t[c0][:, r * P:(r + 1) * P], ident[:])
+
+        def copy_turned(c0):
+            k, o = find(Y_TILES, (c0, P))
+            nc.scalar.copy(out=y32[k][:, :, o:o + P], in_=in_bank[c0 // P][:])
+
+
         def product(out, r, g, h, c0, wd):
-            k, o = holder(PIECES, g, c0, wd)
+            k, o = find(PIECES, (g, c0, wd))
             nc.tensor.matmul_mx(
                 out=out,
                 lhsT=x_codes[g][:, r * P:(r + 1) * P].bitcast(FP8X4),
                 lhsT_scale=x_scales[g][:, r * P:(r + 1) * P],
                 rhs=w_codes[k][:, h, o:o + wd].bitcast(FP8X4),
                 rhs_scale=w_scales[k][:, h, o:o + wd],
-                start=(g == 0 and h == 0), stop=(g == PASSES - 1 and h == 1))
+                start=(g == 0 and h == HI), stop=(g == PASSES - 1 and h == LO))
 
-        def mm_turned(c0, g, bank):
-            k, o = holder(PIECES, g, c0, P)
-            if g == 0:
-                held[bank] = psum.tile([P, T], F32, name="sum_t%d" % c0, tag="bank%d" % bank)
-            for h in range(2):
-                nc.tensor.matmul_mx(
-                    out=held[bank][:],
-                    lhsT=w_codes[k][:, h, o:o + P].bitcast(FP8X4),
-                    lhsT_scale=w_scales[k][:, h, o:o + P],
-                    rhs=x_codes[g][:].bitcast(FP8X4),
-                    rhs_scale=x_scales[g][:],
-                    start=(g == 0 and h == 0), stop=(g == PASSES - 1 and h == 1))
+        def products_in_pairs(c0, bank):
+            for u in range(2):
+                sums = bank_tile(bank + u, [P, 2, 256], "sum%d_%d" % (c0, u))
+                for v in range(2):
+                    for g in range(PASSES):
+                        for h in (HI, LO):
+                            product(sums[:, v, :], 2 * u + v, g, h, c0, 256)
 
-        def drain_turned(c0, bank):
-            y_t = keep.tile([P, T], F32, name="y_t%d" % c0)
-            held[("y_t", c0)] = y_t
-            nc.scalar.activation(out=y_t[:], in_=held[bank][:], func=ACT.Identity,
-                                 bias=b_col[:, c0 // P:c0 // P + 1], scale=1.0)
+        def drain_pair(c0, bank, u):
+            k, o = find(Y_TILES, (c0, 256))
+            bias_cols = bias[:, c0 - TURNED_COLS:c0 - TURNED_COLS + 256]
+            nc.vector.tensor_tensor(out=y32[k][:, 2 * u:2 * u + 2, :], in0=in_bank[bank + u][:],
+                                    in1=bias_cols.unsqueeze(1).to_broadcast([P, 2, 256]), op=ALU.add)
 
-        def turn(c0, bank):
-            held[bank] = psum.tile([P, PACK, P], F32, name="turned%d" % c0, tag="bank%d" % bank)
+        def products_by_row(c0, bank, g, h):
             for r in range(PACK):
-                nc.tensor.transpose(held[bank][:, r, :], held[("y_t", c0)][:, r * P:(r + 1) * P], ident[:])
+                if g == 0 and h == HI:
+                    bank_tile(bank + r, [P, P], "sum_r%d_%d" % (c0, r))
+                product(in_bank[bank + r][:], r, g, h, c0, P)
 
-        def copy_turned(c0, bank):
-            k, o = span(Y_TILES, c0, P)
-            nc.scalar.copy(out=y32[k][:, :, o:o + P], in_=held[bank][:])
-
-        def mm_bank(c0, wd, bank, u):
-            per_bank = 512 // wd
-            held[bank] = psum.tile([P, per_bank, wd], F32, name="sum%d_%d" % (c0, u), tag="bank%d" % bank)
-            for v in range(per_bank):
-                for g in range(PASSES):
-                    for h in range(2):
-                        product(held[bank][:, v, :], u * per_bank + v, g, h, c0, wd)
-
-        def drain_bank(c0, wd, bank, u):
-            per_bank = 512 // wd
-            k, o = span(Y_TILES, c0, wd)
-            nc.vector.tensor_tensor(
-                out=y32[k][:, u * per_bank:(u + 1) * per_bank, o:o + wd], in0=held[bank][:],
-                in1=bias[:, c0 - BIAS0:c0 - BIAS0 + wd].unsqueeze(1).to_broadcast([P, per_bank, wd]), op=ALU.add)
-
-        def mm_rows(c0, wd, bank, g, h):
+        def drain_rows(c0, bank):
+            k, o = find(Y_TILES, (c0, P))
             for r in range(PACK):
-                if g == 0 and h == 0:
-                    held[bank + r] = psum.tile([P, wd], F32, name="sum_r%d_%d" % (c0, r), tag="bank%d" % (bank + r))
-                product(held[bank + r][:], r, g, h, c0, wd)
+                nc.vector.tensor_tensor(out=y32[k][:, r, :], in0=in_bank[bank + r][:],
+                                        in1=bias[:, c0 - TURNED_COLS:c0 - TURNED_COLS + P], op=ALU.add)
 
-        def drain_rows(c0, wd, bank):
-            k, o = span(Y_TILES, c0, wd)
-            for r in range(PACK):
-                nc.vector.tensor_tensor(out=y32[k][:, r, o:o + wd], in0=held[bank + r][:],
-                                        in1=bias[:, c0 - BIAS0:c0 - BIAS0 + wd], op=ALU.add)
 
-        def store_y(c0, wd):
-            k, o = span(Y_TILES, c0, wd)
-            nc.sync.dma_start(out=out_rows[:, :, c0:c0 + wd], in_=y32[k][:])
+        def store_y(c0, wd, rows=slice(0, PACK)):
+            k, o = find(Y_TILES, (c0, wd))
+            nc.sync.dma_start(out=out_rows[:, rows, c0:c0 + wd], in_=y32[k][:, rows, :])
 
-        def cast_y(c0, wd):
-            k, o = span(Y_TILES, c0, wd)
-            kp, op = span(PLANES, c0, wd)
+        def cast_y(c0, wd, eng=nc.scalar):
+            k, o = find(Y_TILES, (c0, wd))
+            kq, oq = find(Y_QUANTS, (c0, wd))
             src = y32[k][:, :, o:o + wd].rearrange("p r (c i) -> p c r i", i=2)
-            nc.scalar.copy(out=paired(y_bf[kp][:, PACK * op:PACK * (op + wd)]), in_=src)
+            copy_on(eng, paired(y_bf[kq][:, PACK * oq:PACK * (oq + wd)]), src)
 
         def quant_y(c0, wd):
-            k, o = span(PLANES, c0, wd)
-            kw, ow = span(WORD_TILES, c0, wd)
-            nc.vector.quantize_mx(out=y_codes[kw][:, ow:ow + wd].bitcast(FP8X4), scales=y_scales[:, c0:c0 + wd], in_=y_bf[k][:])
+            kq, oq = find(Y_QUANTS, (c0, wd))
+            kw, ow = find(WORD_TILES, (c0, wd))
+            nc.vector.quantize_mx(out=y_codes[kw][:, ow:ow + wd].bitcast(FP8X4), scales=y_scales[:, c0:c0 + wd], in_=y_bf[kq][:])
 
-        def store_words(c0, wd, eng):
-            k, o = span(WORD_TILES, c0, wd)
-            eng.dma_start(out=out_words[:, c0:c0 + wd], in_=y_codes[k][:].bitcast(I32))
+        def store_words(c0, wd, eng=nc.sync):
+            kw, ow = find(WORD_TILES, (c0, wd))
+            eng.dma_start(out=out_words[:, c0:c0 + wd], in_=y_codes[kw][:].bitcast(I32))
 
-        def store_scales(c0, c1, two):
+        def store_scales(thirds, engines):
             for q in range(4):
-                eng = nc.scalar if two and q % 2 else nc.sync
-                eng.dma_start(out=out_scales[4 * q:4 * q + 4, c0 // 4:c1 // 4],
-                              in_=y_scales[32 * q:32 * q + 4, c0:c1].bitcast(I32))
+                dst = out_scales[4 * q:4 * q + 4, :].rearrange("r (a n) -> r a n", a=3)
+                src = y_scales[32 * q:32 * q + 4, :].bitcast(I32).rearrange("r (a n) -> r a n", a=3)
+                engines[q % len(engines)].dma_start(out=dst[:, thirds, :], in_=src[:, thirds, :])
 
-        def bias_columns(bank):
-            b_turned = psum.tile([P, P], F32, name="b_turned", tag="bank%d" % bank)
-            nc.tensor.transpose(b_turned[:], b_rows[:], ident[:])
-            nc.scalar.copy(out=b_col[:], in_=b_turned[:, 0:B_COLS])
+        def step(i, mask_next):
+            lower(i)
+            mask(mask_next)
+            quant_both(i)
 
-        def spread(blk, bank):
-            held[bank] = psum.tile([P, 4, P], F32, name="spread%d" % blk, tag="bank%d" % bank)
-            for v in range(4):
-                col = 4 * blk + v
-                nc.tensor.transpose(held[bank][:, v, :], b_col[:, col:col + 1].to_broadcast([P, P]), ident[:])
-
-        def copy_bias(blk, bank):
-            nc.scalar.copy(out=bias[:, 512 * blk - BIAS0:512 * (blk + 1) - BIAS0], in_=held[bank][:].rearrange("q v p -> q (v p)"))
 
         nc.vector.memset(b_rows[:], 0.0)
         make_identity(nc, ident[:])
-        load_w(0)
-        load_w(1)
-        load_w(2)
+
+        for i in range(3):
+            load_w(i)
         load_b()
-        load_w(3)
-        load_w(4)
-        load_w(5)
-        load_w(6)
+        for i in range(3, 6):
+            load_w(i)
         load_x(0)
-        load_w(7)
+        load_w(6)
         load_x(1)
-        load_w(8)
-        load_w(9)
-        load_w(10)
-        load_w(11)
-        load_w(12)
-        load_w(13)
-        upper_v(0)
+        for i in range(7, len(W_LOADS)):
+            load_w(i)
+
+        upper(0, nc.vector)
         mask(0)
-        upper(1)
-        lower(0)
-        mask(1)
-        quant_both(0)
-        upper(2)
-        lower(1)
-        mask(2)
-        quant_both(1)
-        upper(3)
-        lower(2)
-        mask(3)
-        quant_both(2)
+        for i in range(3):
+            upper(i + 1)
+            step(i, i + 1)
         bias_columns(7)
-        spread(1, 5)
-        spread(2, 6)
+        spread_bias(512, 5)
+        spread_bias(1024, 6)
         upper(4)
-        lower(3)
-        mask(4)
-        quant_both(3)
+        step(3, 4)
         upper(5)
-        copy_bias(1, 5)
-        lower(4)
-        mask(5)
-        quant_both(4)
+        copy_bias(512, 5)
+        step(4, 5)
         upper(6)
-        copy_bias(2, 6)
-        lower(5)
-        mask(6)
-        quant_both(5)
+        copy_bias(1024, 6)
+        step(5, 6)
+
         cast_x(0, 0)
         cast_x(0, 1)
         upper(7)
         lower(6)
         quant_x(0)
         quant_both(6)
-        mm_turned(0, 0, 0)
-        mm_turned(128, 0, 1)
-        mm_turned(256, 0, 2)
-        mm_turned(384, 0, 3)
+        for c0 in range(0, TURNED_COLS, P):
+            products_turned(c0, 0)
         mask(7)
         cast_x(1, 0)
-        cast_xv(1, 1)
+        cast_x(1, 1, nc.vector)
         upper(8)
         lower(7)
         quant_x(1)
         mask(8)
         quant_both(7)
-        mm_turned(0, 1, 0)
-        mm_turned(128, 1, 1)
-        mm_turned(256, 1, 2)
-        mm_turned(384, 1, 3)
-        mm_bank(512, 256, 4, 0)
-        mm_bank(512, 256, 5, 1)
+        for c0 in range(0, TURNED_COLS, P):
+            products_turned(c0, 1)
+        products_in_pairs(512, 4)
+
         upper(9)
         upper(10)
-        lower(8)
-        mask(9)
-        quant_both(8)
+        step(8, 9)
         mask(10)
-        drain_turned(0, 0)
+        drain_turned(0)
         upper(11)
-        drain_turned(128, 1)
-        turn(0, 0)
-        turn(128, 1)
-        lower(9)
-        mask(11)
-        quant_both(9)
-        lower_g(11)
-        mm_bank(768, 256, 6, 0)
-        mm_bank(768, 256, 7, 1)
-        drain_bank(512, 256, 4, 0)
-        drain_bank(512, 256, 5, 1)
+        drain_turned(128)
+        turn(0)
+        turn(128)
+        step(9, 11)
+        lower_on_gpsimd(11)
+        products_in_pairs(768, 6)
+        drain_pair(512, 4, 0)
+        drain_pair(512, 4, 1)
         store_y(512, 256)
+
         upper(12)
-        drain_turned(256, 2)
-        drain_turned(384, 3)
-        turn(256, 2)
-        turn(384, 3)
-        copy_turned(0, 0)
-        copy_turned(128, 1)
+        drain_turned(256)
+        drain_turned(384)
+        turn(256)
+        turn(384)
+        copy_turned(0)
+        copy_turned(128)
         store_y(0, 256)
-        lower(10)
-        mask(12)
-        quant_both(10)
-        lower_g(12)
-        drain_bank(768, 256, 6, 0)
-        drain_bank(768, 256, 7, 1)
+        step(10, 12)
+        lower_on_gpsimd(12)
+        drain_pair(768, 6, 0)
+        drain_pair(768, 6, 1)
         store_y(768, 256)
         upper(13)
-        upper(14)
+        upper(LAST)
         cast_y(512, 256)
         cast_y(768, 256)
-        copy_turned(256, 2)
-        copy_turned(384, 3)
+        copy_turned(256)
+        copy_turned(384)
         store_y(256, 256)
         cast_y(0, 256)
         cast_y(256, 256)
-        lower(11)
-        mask(13)
-        quant_both(11)
-        mm_bank(1024, 256, 4, 0)
-        mm_bank(1024, 256, 5, 1)
+        step(11, 13)
+        products_in_pairs(1024, 4)
+
         lower(12)
         quant_y(512, 512)
-        store_words(512, 512, nc.sync)
+        store_words(512, 512)
+        store_scales(slice(1, 2), [nc.sync])
         quant_both(12)
-        mm_rows(1280, 128, 0, 0, 0)
-        mm_rows(1280, 128, 0, 0, 1)
-        lower(13)
-        mask(14)
-        quant_both(13)
-        lower_g(14)
-        mm_rows(1280, 128, 0, 1, 0)
-        mm_rows(1280, 128, 0, 1, 1)
-        drain_bank(1024, 256, 4, 0)
-        drain_bank(1024, 256, 5, 1)
-        store_y(1024, 256)
+        products_by_row(1280, 0, 0, HI)
+        products_by_row(1280, 0, 0, LO)
+        step(13, LAST)
+        lower_on_gpsimd(LAST)
+        products_by_row(1280, 0, 1, HI)
+        products_by_row(1280, 0, 1, LO)
+        for u in range(2):
+            drain_pair(1024, 4, u)
+            store_y(1024, 256, slice(2 * u, 2 * u + 2))
         cast_y(1024, 256)
-        mm_rows(1408, 128, 4, 0, 0)
-        mm_rows(1408, 128, 4, 0, 1)
-        lower(14)
-        quant_part(14, 0)
-        mm_rows(1408, 128, 4, 1, 0)
+        products_by_row(1408, 4, 0, HI)
+        products_by_row(1408, 4, 0, LO)
+
+        lower(LAST)
+        quant_part(LAST, HI)
+        products_by_row(1408, 4, 1, HI)
         quant_y(0, 512)
-        store_words(0, 512, nc.sync)
-        quant_part(14, 1)
-        mm_rows(1408, 128, 4, 1, 1)
-        drain_rows(1280, 128, 0)
+        store_words(0, 512)
+        quant_part(LAST, LO)
+        products_by_row(1408, 4, 1, LO)
+
+        drain_rows(1280, 0)
         store_y(1280, 128)
         cast_y(1280, 128)
-        drain_rows(1408, 128, 4)
+        drain_rows(1408, 4)
         store_y(1408, 128)
-        cast_y(1408, 128)
+        cast_y(1408, 64)
         quant_y(1024, 256)
-        quant_y(1280, 256)
-        store_words(1024, 512, nc.scalar)
-        store_scales(0, 1536, True)
+        cast_y(1472, 64, nc.vector)
+        quant_y(1280, 128)
+        store_words(1024, 384)
+        quant_y(1408, 128)
+        store_words(1408, 128, nc.scalar)
+        store_scales(slice(0, 3, 2), [nc.sync, nc.scalar])

from contextlib import ExitStack

import concourse.mybir as mybir
from concourse.masks import make_identity

K, M, T = 1024, 1536, 512
FLOPS = 2 * 2 * K * M * T

F32 = mybir.dt.float32
BF16 = mybir.dt.bfloat16
I32 = mybir.dt.int32
U32 = mybir.dt.uint32
U8 = mybir.dt.uint8
FP8X4 = mybir.dt.float8_e4m3fn_x4
ALU = mybir.AluOpType
ACT = mybir.ActivationFunctionType

P = 128
PACK = 4
K_PASS = P * PACK
PASSES = K // K_PASS
BANK = 512
HI, LO = 0, 1
HI_MASK_PAIR = 0xFFF0FFF0 - (1 << 32)
B_ROWS = M // P
TURNED_COLS = 512

W_LOADS = [(0, 0, 128), (0, 128, 128), (0, 256, 256), (1, 0, 256), (1, 256, 256)] + [
    (g, c0, 256) for c0 in range(TURNED_COLS, M, 256) for g in range(PASSES)
]
PIECES = W_LOADS[:2] + [(0, 256, 128), (0, 384, 128)] + W_LOADS[3:-1] + [(1, 1280, 128), (1, 1408, 128)]
LAST = len(PIECES) - 1
GPSIMD_COLS = {11: 80, 12: 80, LAST: 80}
Y_TILES = [(c0, 256) for c0 in range(0, 1280, 256)] + [(1280, 128), (1408, 128)]
Y_QUANTS = [(0, 512), (512, 512), (1024, 256), (1280, 128), (1408, 128)]
WORD_TILES = [(0, 512), (512, 512), (1024, 384), (1408, 128)]


def find(ranges, key):
    c0, wd = key[-2:]
    return [
        (i, c0 - entry[-2])
        for i, entry in enumerate(ranges)
        if entry[:-2] == key[:-2] and entry[-2] <= c0 and c0 + wd <= entry[-2] + entry[-1]
    ][0]


def paired(packed):
    return packed.rearrange("p (c i j) -> p c j i", i=2, j=PACK)


def tile_mix_hilo_tm_pl_bias_kernel(tc, w, x, b, out_0, out_1, out_2):
    nc = tc.nc
    out_rows = out_0.rearrange("(p r) n -> p r n", r=PACK)
    out_words = out_1.rearrange("a p n i -> (a p) (n i)").bitcast(I32)
    out_scales = out_2.rearrange("a q n -> (a q) n").bitcast(I32)

    with ExitStack() as ctx:
        keep = ctx.enter_context(tc.tile_pool(name="keep", bufs=1))
        psum = ctx.enter_context(tc.psum_pool(name="psum", bufs=1))
        ctx.enter_context(tc.manual_schedule())

        ident = keep.tile([P, P], F32, name="ident")
        b_rows = keep.tile([P, P], F32, name="b_rows")
        b_col = keep.tile([P, B_ROWS], F32, name="b_col")
        bias = keep.tile([P, M - TURNED_COLS], F32, name="bias")
        w_raw = [keep.tile([P, PACK, wd], F32, name="w_raw%d" % i) for i, (g, c0, wd) in enumerate(W_LOADS)]
        x_raw = [keep.tile([P, PACK, T], F32, name="x_raw%d" % g) for g in range(PASSES)]
        x_bf = [keep.tile([P, PACK * T], BF16, name="x_bf%d" % g, align_bytes=64) for g in range(PASSES)]
        x_codes = [keep.tile([P, T], U32, name="x_codes%d" % g, align_bytes=64) for g in range(PASSES)]
        x_scales = [keep.tile([P, T], U8, name="x_scales%d" % g, align_bytes=64) for g in range(PASSES)]
        w_bf = [keep.tile([P, 2, PACK * wd], BF16, name="w_bf%d" % i, align_bytes=64) for i, (g, c0, wd) in enumerate(PIECES)]
        w_codes = [keep.tile([P, 2, wd], U32, name="w_codes%d" % i, align_bytes=64) for i, (g, c0, wd) in enumerate(PIECES)]
        w_scales = [keep.tile([P, 2, wd], U8, name="w_scales%d" % i, align_bytes=64) for i, (g, c0, wd) in enumerate(PIECES)]
        y32 = [keep.tile([P, PACK, wd], F32, name="y32_%d" % i) for i, (c0, wd) in enumerate(Y_TILES)]
        y_bf = [keep.tile([P, PACK * wd], BF16, name="y_bf%d" % i, align_bytes=64) for i, (c0, wd) in enumerate(Y_QUANTS)]
        y_codes = [keep.tile([P, wd], U32, name="y_codes%d" % i, align_bytes=64) for i, (c0, wd) in enumerate(WORD_TILES)]
        y_scales = keep.tile([P, M], U8, name="y_scales", align_bytes=64)
        in_bank = {}
        y_t = {}

        def bank_tile(bank, shape, name):
            in_bank[bank] = psum.tile(shape, F32, name=name, tag="bank%d" % bank)
            return in_bank[bank]

        def copy_on(eng, out, in_):
            if eng is nc.scalar:
                nc.scalar.copy(out=out, in_=in_)
            else:
                nc.vector.tensor_copy(out=out, in_=in_)


        def load_w(i):
            g, c0, wd = W_LOADS[i]
            rows = w[g * K_PASS:(g + 1) * K_PASS, c0:c0 + wd]
            nc.sync.dma_start(out=w_raw[i][:], in_=rows.rearrange("(p j) n -> p j n", j=PACK))

        def load_x(g):
            rows = x[g * K_PASS:(g + 1) * K_PASS, :]
            nc.sync.dma_start(out=x_raw[g][:], in_=rows.rearrange("(p j) t -> p j t", j=PACK))

        def upper(i, eng=nc.scalar):
            k, o = find(W_LOADS, PIECES[i])
            halves = w_raw[k][:].bitcast(BF16)[:, :, 2 * o:2 * (o + PIECES[i][2])]
            halves = halves.rearrange("p j (c i h) -> p c j i h", i=2, h=2)
            copy_on(eng, paired(w_bf[i][:, HI, :]), halves[:, :, :, :, 1])

        def mask(i):
            words = w_bf[i][:, HI, :].bitcast(I32)
            nc.vector.tensor_scalar(out=words, in0=words, scalar1=HI_MASK_PAIR, scalar2=None, op0=ALU.bitwise_and)

        def subtract(eng, i, first, end):
            k, o = find(W_LOADS, PIECES[i])
            src = w_raw[k][:, :, o + first:o + end].rearrange("p j (c i) -> p c j i", i=2)
            eng.tensor_tensor(out=paired(w_bf[i][:, LO, PACK * first:PACK * end]), in0=src,
                              in1=paired(w_bf[i][:, HI, PACK * first:PACK * end]), op=ALU.subtract)

        def lower(i):
            subtract(nc.vector, i, 0, PIECES[i][2] - GPSIMD_COLS.get(i, 0))

        def lower_on_gpsimd(i):
            subtract(nc.gpsimd, i, PIECES[i][2] - GPSIMD_COLS[i], PIECES[i][2])

        def quant_part(i, h):
            nc.vector.quantize_mx(out=w_codes[i][:, h, :].bitcast(FP8X4), scales=w_scales[i][:, h, :], in_=w_bf[i][:, h, :])

        def quant_both(i):
            nc.vector.quantize_mx(out=w_codes[i][:].rearrange("p h n -> p (h n)").bitcast(FP8X4),
                                  scales=w_scales[i][:].rearrange("p h n -> p (h n)"),
                                  in_=w_bf[i][:].rearrange("p h n -> p (h n)"))

        def cast_x(g, half, eng=nc.scalar):
            dst = x_bf[g][:].rearrange("p (u v m j) -> p u m j v", u=2, v=2, j=PACK)
            src = x_raw[g][:].rearrange("p j (m u v) -> p u m j v", u=2, v=2)
            copy_on(eng, dst[:, half], src[:, half])

        def quant_x(g):
            nc.vector.quantize_mx(out=x_codes[g][:].bitcast(FP8X4), scales=x_scales[g][:], in_=x_bf[g][:])


        def load_b():
            nc.sync.dma_start(out=b_rows[0:B_ROWS, :], in_=b.rearrange("(c p) -> c p", p=P))

        def bias_columns(bank):
            b_turned = bank_tile(bank, [P, P], "b_turned")
            nc.tensor.transpose(b_turned[:], b_rows[:], ident[:])
            nc.scalar.copy(out=b_col[:], in_=b_turned[:, 0:B_ROWS])

        def spread_bias(c0, bank):
            spread = bank_tile(bank, [P, BANK // P, P], "spread%d" % c0)
            for v in range(BANK // P):
                col = c0 // P + v
                nc.tensor.transpose(spread[:, v, :], b_col[:, col:col + 1].to_broadcast([P, P]), ident[:])

        def copy_bias(c0, bank):
            nc.scalar.copy(out=bias[:, c0 - TURNED_COLS:c0 - TURNED_COLS + BANK],
                           in_=in_bank[bank][:].rearrange("q v p -> q (v p)"))


        def products_turned(c0, g):
            k, o = find(PIECES, (g, c0, P))
            if g == 0:
                bank_tile(c0 // P, [P, T], "sum_t%d" % c0)
            for h in (HI, LO):
                nc.tensor.matmul_mx(
                    out=in_bank[c0 // P][:],
                    lhsT=w_codes[k][:, h, o:o + P].bitcast(FP8X4),
                    lhsT_scale=w_scales[k][:, h, o:o + P],
                    rhs=x_codes[g][:].bitcast(FP8X4),
                    rhs_scale=x_scales[g][:],
                    start=(g == 0 and h == HI), stop=(g == PASSES - 1 and h == LO))

        def drain_turned(c0):
            y_t[c0] = keep.tile([P, T], F32, name="y_t%d" % c0)
            nc.scalar.activation(out=y_t[c0][:], in_=in_bank[c0 // P][:], func=ACT.Identity,
                                 bias=b_col[:, c0 // P:c0 // P + 1], scale=1.0)

        def turn(c0):
            turned = bank_tile(c0 // P, [P, PACK, P], "turned%d" % c0)
            for r in range(PACK):
                nc.tensor.transpose(turned[:, r, :], y_t[c0][:, r * P:(r + 1) * P], ident[:])

        def copy_turned(c0):
            k, o = find(Y_TILES, (c0, P))
            nc.scalar.copy(out=y32[k][:, :, o:o + P], in_=in_bank[c0 // P][:])


        def product(out, r, g, h, c0, wd):
            k, o = find(PIECES, (g, c0, wd))
            nc.tensor.matmul_mx(
                out=out,
                lhsT=x_codes[g][:, r * P:(r + 1) * P].bitcast(FP8X4),
                lhsT_scale=x_scales[g][:, r * P:(r + 1) * P],
                rhs=w_codes[k][:, h, o:o + wd].bitcast(FP8X4),
                rhs_scale=w_scales[k][:, h, o:o + wd],
                start=(g == 0 and h == HI), stop=(g == PASSES - 1 and h == LO))

        def products_in_pairs(c0, bank):
            for u in range(2):
                sums = bank_tile(bank + u, [P, 2, 256], "sum%d_%d" % (c0, u))
                for v in range(2):
                    for g in range(PASSES):
                        for h in (HI, LO):
                            product(sums[:, v, :], 2 * u + v, g, h, c0, 256)

        def drain_pair(c0, bank, u):
            k, o = find(Y_TILES, (c0, 256))
            bias_cols = bias[:, c0 - TURNED_COLS:c0 - TURNED_COLS + 256]
            nc.vector.tensor_tensor(out=y32[k][:, 2 * u:2 * u + 2, :], in0=in_bank[bank + u][:],
                                    in1=bias_cols.unsqueeze(1).to_broadcast([P, 2, 256]), op=ALU.add)

        def products_by_row(c0, bank, g, h):
            for r in range(PACK):
                if g == 0 and h == HI:
                    bank_tile(bank + r, [P, P], "sum_r%d_%d" % (c0, r))
                product(in_bank[bank + r][:], r, g, h, c0, P)

        def drain_rows(c0, bank):
            k, o = find(Y_TILES, (c0, P))
            for r in range(PACK):
                nc.vector.tensor_tensor(out=y32[k][:, r, :], in0=in_bank[bank + r][:],
                                        in1=bias[:, c0 - TURNED_COLS:c0 - TURNED_COLS + P], op=ALU.add)


        def store_y(c0, wd, rows=slice(0, PACK)):
            k, o = find(Y_TILES, (c0, wd))
            nc.sync.dma_start(out=out_rows[:, rows, c0:c0 + wd], in_=y32[k][:, rows, :])

        def cast_y(c0, wd, eng=nc.scalar):
            k, o = find(Y_TILES, (c0, wd))
            kq, oq = find(Y_QUANTS, (c0, wd))
            src = y32[k][:, :, o:o + wd].rearrange("p r (c i) -> p c r i", i=2)
            copy_on(eng, paired(y_bf[kq][:, PACK * oq:PACK * (oq + wd)]), src)

        def quant_y(c0, wd):
            kq, oq = find(Y_QUANTS, (c0, wd))
            kw, ow = find(WORD_TILES, (c0, wd))
            nc.vector.quantize_mx(out=y_codes[kw][:, ow:ow + wd].bitcast(FP8X4), scales=y_scales[:, c0:c0 + wd], in_=y_bf[kq][:])

        def store_words(c0, wd, eng=nc.sync):
            kw, ow = find(WORD_TILES, (c0, wd))
            eng.dma_start(out=out_words[:, c0:c0 + wd], in_=y_codes[kw][:].bitcast(I32))

        def store_scales(thirds, engines):
            for q in range(4):
                dst = out_scales[4 * q:4 * q + 4, :].rearrange("r (a n) -> r a n", a=3)
                src = y_scales[32 * q:32 * q + 4, :].bitcast(I32).rearrange("r (a n) -> r a n", a=3)
                engines[q % len(engines)].dma_start(out=dst[:, thirds, :], in_=src[:, thirds, :])

        def step(i, mask_next):
            lower(i)
            mask(mask_next)
            quant_both(i)


        nc.vector.memset(b_rows[:], 0.0)
        make_identity(nc, ident[:])

        for i in range(3):
            load_w(i)
        load_b()
        for i in range(3, 6):
            load_w(i)
        load_x(0)
        load_w(6)
        load_x(1)
        for i in range(7, len(W_LOADS)):
            load_w(i)

        upper(0, nc.vector)
        mask(0)
        for i in range(3):
            upper(i + 1)
            step(i, i + 1)
        bias_columns(7)
        spread_bias(512, 5)
        spread_bias(1024, 6)
        upper(4)
        step(3, 4)
        upper(5)
        copy_bias(512, 5)
        step(4, 5)
        upper(6)
        copy_bias(1024, 6)
        step(5, 6)

        cast_x(0, 0)
        cast_x(0, 1)
        upper(7)
        lower(6)
        quant_x(0)
        quant_both(6)
        for c0 in range(0, TURNED_COLS, P):
            products_turned(c0, 0)
        mask(7)
        cast_x(1, 0)
        cast_x(1, 1, nc.vector)
        upper(8)
        lower(7)
        quant_x(1)
        mask(8)
        quant_both(7)
        for c0 in range(0, TURNED_COLS, P):
            products_turned(c0, 1)
        products_in_pairs(512, 4)

        upper(9)
        upper(10)
        step(8, 9)
        mask(10)
        drain_turned(0)
        upper(11)
        drain_turned(128)
        turn(0)
        turn(128)
        step(9, 11)
        lower_on_gpsimd(11)
        products_in_pairs(768, 6)
        drain_pair(512, 4, 0)
        drain_pair(512, 4, 1)
        store_y(512, 256)

        upper(12)
        drain_turned(256)
        drain_turned(384)
        turn(256)
        turn(384)
        copy_turned(0)
        copy_turned(128)
        store_y(0, 256)
        step(10, 12)
        lower_on_gpsimd(12)
        drain_pair(768, 6, 0)
        drain_pair(768, 6, 1)
        store_y(768, 256)
        upper(13)
        upper(LAST)
        cast_y(512, 256)
        cast_y(768, 256)
        copy_turned(256)
        copy_turned(384)
        store_y(256, 256)
        cast_y(0, 256)
        cast_y(256, 256)
        step(11, 13)
        products_in_pairs(1024, 4)

        lower(12)
        quant_y(512, 512)
        store_words(512, 512)
        store_scales(slice(1, 2), [nc.sync])
        quant_both(12)
        products_by_row(1280, 0, 0, HI)
        products_by_row(1280, 0, 0, LO)
        step(13, LAST)
        lower_on_gpsimd(LAST)
        products_by_row(1280, 0, 1, HI)
        products_by_row(1280, 0, 1, LO)
        for u in range(2):
            drain_pair(1024, 4, u)
            store_y(1024, 256, slice(2 * u, 2 * u + 2))
        cast_y(1024, 256)
        products_by_row(1408, 4, 0, HI)
        products_by_row(1408, 4, 0, LO)

        lower(LAST)
        quant_part(LAST, HI)
        products_by_row(1408, 4, 1, HI)
        quant_y(0, 512)
        store_words(0, 512)
        quant_part(LAST, LO)
        products_by_row(1408, 4, 1, LO)

        drain_rows(1280, 0)
        store_y(1280, 128)
        cast_y(1280, 128)
        drain_rows(1408, 4)
        store_y(1408, 128)
        cast_y(1408, 64)
        quant_y(1024, 256)
        cast_y(1472, 64, nc.vector)
        quant_y(1280, 128)
        store_words(1024, 384)
        quant_y(1408, 128)
        store_words(1408, 128, nc.scalar)
        store_scales(slice(0, 3, 2), [nc.sync, nc.scalar])
